import numpy as np, ml_dtypes
CORES = [3,11,19,27,35,43,51,59]
N = 8
import mx_ref
BF = ml_dtypes.bfloat16
def pick(q, e):
    c = np.concatenate([q[0].reshape(128, -1, 4), np.zeros((128, 1, 4), np.uint8)], axis=1); s = np.concatenate([q[1], np.ones((16, 1), np.uint8)], axis=1)
    return (np.ascontiguousarray(c[:, e].reshape(128, -1)), np.ascontiguousarray(s[:, e]))
def join(*qs):
    return (np.concatenate([q[0] for q in qs], axis=1), np.concatenate([q[1] for q in qs], axis=1))
def put(q, e, v):
    c, s = q[0].reshape(128, -1, 4).copy(), q[1].copy(); c[:, e] = v[0].reshape(128, -1, 4); s[:, e] = v[1]
    return (c.reshape(128, -1), s)
def pk(c, s):
    return (np.ascontiguousarray(c), mx_ref.live(s))
def emit(q):
    return q[0], q[1]
def decode(q):
    o = []
    for b in range(4):
        e = np.zeros((128, 128, 4), np.float32); e[np.arange(128), np.arange(128), b] = 1
        o.append(mx_ref.matmul(mx_ref.quantize(e.reshape(128, 512).astype(BF)), q))
    return np.stack(o, axis=2).reshape(128, -1)
def cols(t, e):
    v = np.concatenate([t.reshape(128, -1, 4), np.zeros((128, 1, 4), BF)], axis=1)
    return np.ascontiguousarray(v[:, e]).reshape(128, -1)
def cut(t, i, w=512):
    return t[:, w * i:w * i + w]
def f(rng, *shape):
    return mx_ref.flush((rng.standard_normal(shape, dtype=np.float32) * np.exp2(rng.integers(-2, 3, shape[:-1] + (1,)))).astype(BF))
def wide(rng, *shape, cols=0):
    v = rng.standard_normal(shape, dtype=np.float32) * np.exp2(rng.integers(-12, 13, shape)).astype(np.float32)
    if cols: v *= np.repeat(np.exp2(rng.integers(-cols, cols + 1, shape[:-2] + (1, shape[-1] // 4))) * (rng.random(shape[:-2] + (1, shape[-1] // 4)) > 0.0625), 4, axis=-1).astype(np.float32)
    return mx_ref.flush(v.astype(BF))
C, T, R, O = 256, 64, 3, 1
def trim(v):
    v = v.astype(np.float32)
    v[np.abs(v) < np.float32(2.0 ** -14)] = 0
    return v.astype(BF)
def given(rng, u, x):
    return {"kb": np.stack([trim(u.reshape(128, 4 * C))] * N), "x": trim(x.reshape(N, 128, 4 * R * T)), "w": f(rng, N, 128, 512 * O)}
def sturdy(rng, n):
    return (1 + rng.random((128, n, 4))) * rng.choice([-1.0, 1.0], (128, n, 4)) * np.exp2(rng.integers(-1, 2, (128, 1, 1)))
def kept(v):
    m, e = np.frexp(v)
    return np.ldexp(np.trunc(m * 8) * 0.125, e)
def near(rng, u, e):
    return u[:, e] + 0.5 * sturdy(rng, len(e))
def setup_inputs(rng):
    return given(rng, f(rng, 128, 4 * C), f(rng, N, 128, 4 * R * T))
def setup_inputs_both(rng):
    u, x, new = kept(sturdy(rng, C)), np.zeros((N, 128, R, T, 4)), np.zeros((N, C), bool)
    for b in range(R):
        for j, r in enumerate(rng.permutation([v for v in range(N) if v < v ^ (1 << b)])):
            p, e = r ^ (1 << b), rng.permutation(C)
            if j % 2: e = e[np.argsort(new[r, e] | ~new[p, e], kind="stable")]
            t = e[T:2 * T] if j % 2 else rng.permutation(e[:T])
            x[r, :, b] = near(rng, u, e[:T])
            x[r, :, b, :T // 4] = u[:, e[:T // 4]]
            x[p, :, b] = near(rng, u, t)
            for s in (r, p):
                new[s, e[:T]] = True
                new[s, t] = True
    return given(rng, u, x)
def setup_inputs_few(rng):
    u, x, four = sturdy(rng, C), np.zeros((N, 128, R, T, 4)), rng.permutation(C)[:4]
    for b in range(R):
        for j, r in enumerate(rng.permutation([v for v in range(N) if v < v ^ (1 << b)])):
            a = rng.permutation(four)[:2]
            for s, c in ((r, a[0]), (r ^ (1 << b), a[j % 2])):
                x[s, :, b] = near(rng, u, np.full(T, c)) * np.exp2(rng.integers(-1, 2, (1, T, 1)))
    return given(rng, u, x)
def setup_inputs_ties(rng):
    u = np.abs(cols(f(rng, 128, 4 * (C // 4)), rng.permutation(np.arange(C) % (C // 4))).astype(np.float32))
    x = np.abs(f(rng, N, 128, 4 * R * T).astype(np.float32)).reshape(N, 128, R, T, 4)
    for r in range(N):
        for b in range(R):
            x[r, :, b] *= (1 - 2 * (rng.permutation(T) % 2)).astype(np.float32)[:, None]
            x[r, :, b, int(rng.integers(0, T))] = 0
    return given(rng, u * np.float32(2.0 ** 18), x * np.float32(2.0 ** 18))
def setup_inputs_drift(rng):
    top = (rng.permutation(128) < 64)[:, None, None]
    u, z, x = sturdy(rng, C) * top, sturdy(rng, 8) * ~top, np.zeros((N, 128, R, T, 4))
    e = rng.permutation(C)
    for r in range(N):
        for b in range(R):
            t = rng.permutation(e[:C // 2] if b == 0 else e[C // 2:])[:T]
            x[r, :, b] = near(rng, u, t) * top + 8 * z[:, rng.permutation(np.arange(T) % 8)]
    return given(rng, u, x)
def setup_inputs_spread(rng):
    d = given(rng, wide(rng, 128, 4 * C, cols=2), wide(rng, N, 128, 4 * R * T, cols=6))
    d["kb"][:, :, :4] = BF(-0.0)
    for r in range(N):
        for b in range(R):
            i = 4 * (b * T + int(rng.integers(0, T)))
            d["x"][r, :, i:i + 4] = BF(0.0)
    return d
def check_inputs(d):
    b = []
    for n, lo, hi in (("kb", -14, 24), ("x", -14, 24), ("w", -30, 30)):
        v = np.abs(d[n].astype(np.float32))
        if not (np.isfinite(v).all() and ((v == 0) | (v >= 2.0 ** lo) & (v <= 2.0 ** hi)).all()): b.append("a value of " + n)
    if (d["kb"].astype(np.float32) != d["kb"][:1].astype(np.float32)).any(): b.append("kb isn't the same on all ranks")
    return b
def numbers(k, e):
    return decode(pick(k, np.concatenate([e, np.full(-len(e) % 4, -1)]))).reshape(128, -1, 4)[:, :len(e)]
def anew(k, e, v):
    t = np.zeros((128, len(e) + -len(e) % 4, 4), np.float32)
    t[:, :len(e)] = v
    return put(k, e, pick(mx_ref.quantize(t.reshape(128, -1).astype(BF)), np.arange(len(e))))
def reference(kb, x, w):
    k = join(*[mx_ref.quantize(np.ascontiguousarray(kb[r])) for r in range(N)])
    q = join(*[mx_ref.quantize(np.ascontiguousarray(x[r])) for r in range(N)])
    dx = decode(q).reshape(128, N, R, T, 4)
    ch = np.zeros((N, R, T), np.float32)
    for b in range(R):
        won, e, t = np.zeros((N, C), bool), [], []
        for r in range(N):
            v = pick(q, (r * R + b) * T + np.arange(T))
            s = np.concatenate([mx_ref.matmul(pick(k, C * r + 128 * m + np.arange(128)), v) for m in range(C // 128)])
            win = np.argmax(s + np.float32(0), axis=0)
            u, i = np.unique(win, return_index=True)
            won[r, u] = True
            e.append(C * r + u)
            t.append(dx[:, r, b, i])
            ch[r, b] = win
        e = np.concatenate(e)
        k = anew(k, e, np.float32(0.75) * numbers(k, e) + np.float32(0.25) * np.concatenate(t, axis=1))
        src, low, high = np.arange(N * C).reshape(N, C), [], []
        for r in range(N):
            p = r ^ (1 << b)
            src[r] = np.where(won[p] & ~won[r], C * p + np.arange(C), src[r])
            if r < p:
                u = np.flatnonzero(won[r] & won[p])
                low.append(C * r + u)
                high.append(C * p + u)
        low, high = np.concatenate(low), np.concatenate(high)
        if len(low):
            v = np.float32(0.5) * numbers(k, low) + np.float32(0.5) * numbers(k, high)
            k = anew(k, np.concatenate([low, high]), np.concatenate([v, v], axis=1))
        k = pick(k, src.reshape(-1))
    oc, osc, y = np.zeros((N, 128, 4 * C), np.uint8), np.zeros((N, 16, C), np.uint8), np.zeros((N, 128, O * C), np.float32)
    for r in range(N):
        t = pick(k, C * r + np.arange(C))
        oc[r], osc[r] = emit(t)
        for o in range(O): y[r, :, C * o:C * o + C] = mx_ref.matmul(mx_ref.quantize(np.ascontiguousarray(cut(w[r], o))), t)
    return {"oc": oc, "osc": osc, "ch": ch, "y": y}

@@ -1,0 +1,278 @@
+from concourse.mybir import dt, AluOpType, ActivationFunctionType
+
+ALU = AluOpType
+ACTF = ActivationFunctionType
+R = 3
+NT = 64
+
+X4 = "float8_e4m3fn_x4"
+SCRATCH = {"ps": ("psum", [128, 1024], "float32"), "pd": ("psum", [128, 2048], "float32"), "pe": ("psum", [128, 1024], "float32"),
+           "pidx": ("sbuf", [128, 1], "int32"), "pand": ("sbuf", [128, 1], "int32")}
+for _n, _w in (("xt", 1024), ("kt", 1024), ("wt", 512), ("z1", 516), ("hs", 512), ("hm", 512), ("hz", 516), ("sg0", 256), ("sg1", 256)):
+    SCRATCH[_n] = ("sbuf", [128, _w], "bfloat16")
+for _n, _w in (("qc", 1), ("qm", 1), ("repi", 16), ("c16", 256), ("row", 384), ("iq", 260), ("mk", 260), ("diag", 256),
+               ("diagn", 32), ("rs", 256), ("base", 256), ("neg", 256), ("jmk", 256), ("step", 80), ("pm0", 256), ("pm1", 256),
+               ("tinb", 64), ("tina", 64), ("toutb", 64), ("touta", 64), ("wrb", 64), ("wra", 64), ("eqb", 260), ("eqa", 260),
+               ("eqj", 256), ("dsb", 260), ("dsa", 260), ("dsj", 256), ("ra", 64), ("t3", 64), ("va", 64), ("vd", 64),
+               ("ls", 256), ("yt", 256), ("dk0", 256), ("dk1", 256), ("dk2", 256), ("dk3", 256),
+               ("tk0", 192), ("tk1", 192), ("tk2", 192), ("tk3", 192)):
+    SCRATCH[_n] = ("sbuf", [128, _w], "float32")
+for _n, _w in (("e1", 512), ("xq", 256), ("wq", 128), ("k3", 256)):
+    SCRATCH[_n] = ("sbuf", [128, _w], X4)
+    SCRATCH[_n + "s"] = ("sbuf", [128, _w], "uint8")
+for _b in range(R):
+    for _n, _w in (("win", 640), ("pj", 128), ("tr", 256)):
+        SCRATCH["%s%d" % (_n, _b)] = ("sbuf", [128, _w], X4)
+        SCRATCH["%ss%d" % (_n, _b)] = ("sbuf", [128, _w], "uint8")
+    for _n, _w in (("rep", 16), ("wb", 4), ("wa", 4), ("ub", 4), ("ua", 4), ("jl", 4), ("ll", 16)):
+        SCRATCH["%s%d" % (_n, _b)] = ("sbuf", [128, _w], "uint16")
+    for _n, _w in (("ml", 320), ("rb", 64), ("wcb", 2), ("wca", 2)):
+        SCRATCH["%s%d" % (_n, _b)] = ("sbuf", [128, _w], "float32")
+
+SEMAPHORES = ["cv", "ca", "cp", "cg", "lx0", "lx1", "lk", "lw", "st", "loc"]
+for _b in range(R):
+    SEMAPHORES += ["rl%d" % _b, "rd%d" % _b]
+
+
+def rank_program(g, core, T, topo):
+    rank = T.rank_of(core)
+    if rank is None:
+        return
+    queues = {"V": (g.vector, "cv"), "A": (g.scalar, "ca"), "P": (g.tensor, "cp"), "G": (g, "cg"), "S": (g.sync, None)}
+    issued = {"cv": 0, "ca": 0, "cp": 0, "cg": 0}
+    known = {q: {} for q in queues}
+
+    def need(q, deps):
+        for sem, val, through in deps:
+            if known[q].get(sem, 0) < val:
+                queues[q][0].wait_ge(T.sem[sem], val)
+                known[q][sem] = val
+                for s, v in through.items():
+                    known[q][s] = max(known[q].get(s, 0), v)
+
+    def do(q, deps, fn, *args, **kw):
+        need(q, deps)
+        sem = queues[q][1]
+        issued[sem] += 1
+        fn(*args, **kw).then_inc(T.sem[sem], 1)
+        return (sem, issued[sem], dict(known[q]))
+
+    def dma(q, deps, sem, out, in_):
+        need(q, deps)
+        queues[q][0].dma_start(out, in_).then_inc(T.sem[sem], 16)
+        return (sem, 16, dict(known[q]))
+
+    vec, act, ten = g.vector, g.scalar, g.tensor
+
+    def V(deps, fn, *args, **kw):
+        return do("V", deps, fn, *args, **kw)
+
+    def A(deps, out, in_, func=ACTF.Copy, **kw):
+        return do("A", deps, act.activation, out, in_, func, **kw)
+
+    def mx(deps, bank, st, a, mv, c, n, start=True, stop=True):
+        return do("P", deps, ten.matmul_mx, bank, T[st[0]][:, a:a + 128], T[st[1]][:, a:a + 128],
+                  T[mv[0]][:, c:c + n], T[mv[1]][:, c:c + n], start, stop)
+
+    def pd(t, a, b):
+        return T.pd[:, 512 * t + a:512 * t + b]
+
+    def px(t, a, b):
+        return (T.ps, T.pe)[t // 2][:, 512 * (t % 2) + a:512 * (t % 2) + b]
+
+    def w8(name, a, b):
+        return T[name][:, a:b].bitcast(dt.uint8)
+
+    def w32(name, a, b):
+        return T[name][:, a:b].bitcast(dt.uint32)
+
+    def pick(out, a, b, win, c, d, off, deps):
+        tc = V(deps, vec.tensor_copy, w32(out[0], a, b), w32(win[0], c, d).indirect(off))
+        ts = A(deps, T[out[1]][:, a:b], T[win[1]][:, c:d].indirect(off))
+        return [tc, ts]
+
+    E1, XQ = ("e1", "e1s"), ("xq", "xqs")
+
+    lx0 = dma("S", [], "lx0", T.xt[:, 0:256], T.x[:, 0:256])
+    lk = dma("A", [], "lk", T.kt[:], T.kb[:])
+    lx1 = dma("S", [], "lx1", T.xt[:, 512:1024], T.x[:, 256:768])
+    lw = dma("S", [], "lw", T.wt[:], T.w[:])
+
+    t_z0 = V([], vec.memset, T.z1[:], 0.0)
+    t_pidx = do("G", [], g.iota, T.pidx[:], [[0, 1]], 0, 1)
+    t_repi = do("G", [], g.iota, T.repi[:], [[32, 2], [0, 4], [16, 2]], 0, 0, allow_small_or_imprecise_dtypes=True)
+    t_z1 = do("G", [t_z0], g.affine_select, T.z1[:, 3:515:4], T.z1[:, 3:515:4], [[-1, 128]], ALU.not_equal, 1.0, 0, 1)
+    t_c16 = do("G", [], g.iota, T.c16[:], [[0, 16], [1, 16]], 0, 0, allow_small_or_imprecise_dtypes=True)
+    t_row = do("G", [], g.iota, T.row[:], [[1, 384]], 0, 0, allow_small_or_imprecise_dtypes=True)
+    t_iq = do("G", [], g.iota, T.iq[:], [[-16, 4], [1, 65]], 0, 0, allow_small_or_imprecise_dtypes=True)
+
+    t_hz = V([], vec.memset, T.hz[:], 0.0)
+    t_xz = A([t_hz], T.xt[:, 256:512], T.hz[:, 0:256])
+    t_and = V([t_pidx], vec.tensor_scalar, T.pand[:], T.pidx[:], 15, None, ALU.bitwise_and)
+    t_q = V([t_and], vec.tensor_copy, T.qc[:], T.pand[:])
+    t_neg = A([t_hz], T.neg[:], T.hz[:, 0:256], ACTF.Copy, bias=-1.0e29)
+    t_jm = [A([t_hz], T.jmk[:], T.hz[:, 0:256], ACTF.Copy, bias=-1.0)]
+    t_jm.append(A(t_jm, T.jmk[:, 0:256:64], T.hz[:, 0:4], ACTF.Copy, bias=100000.0))
+    t_rep, t_pj, t_e1 = {}, {}, []
+
+    def make_rep(b):
+        t_rep[b] = V([t_q, t_repi], vec.tensor_scalar, T["rep%d" % b][:], T.repi[:], T.qc[:], float((0, 128, 192)[b]), ALU.add, ALU.add)
+
+    def make_pj(b):
+        t_pj[b] = V([t_hz], vec.quantize_mx, T["pj%d" % b][:], T["pjs%d" % b][:], T.hz[:, 0:512])
+
+    t_tr = [[] for _ in range(2 * R)]
+    t_tk = {}
+
+    def tr_codes(b, h, dep):
+        t_tr[2 * b + h].append(V([dep, t_rep[b]], vec.tensor_copy, w32("tr%d" % b, 128 * h, 128 * h + 128),
+                                 w32("xq", 0, 256 if b else 128).indirect(T["rep%d" % b][:, 8 * h:8 * h + 8])))
+
+    def tr_scales(b, h, dep):
+        t_tr[2 * b + h].append(A([dep, t_rep[b]], T["trs%d" % b][:, 128 * h:128 * h + 128],
+                                 T.xqs[:, 0:256 if b else 128].indirect(T["rep%d" % b][:, 8 * h:8 * h + 8])))
+
+    make_rep(0)
+    t_x0 = V([lx0, t_xz], vec.quantize_mx, T.xq[:, 0:128], T.xqs[:, 0:128], T.xt[:, 0:512])
+    for i in range(4):
+        t_e1.append(V([t_z1], vec.quantize_mx, T.e1[:, 128 * i:128 * i + 128], T.e1s[:, 128 * i:128 * i + 128], T.z1[:, 3 - i:515 - i]))
+    tr_codes(0, 0, t_x0)
+    for h in range(2):
+        tr_scales(0, h, t_x0)
+    t_tab = [V([lk], vec.quantize_mx, T.win0[:, 0:256], T.wins0[:, 0:256], T.kt[:])]
+    tr_codes(0, 1, t_x0)
+    t_tkm = [mx([t_x0, t_e1[t]], pd(t, 0, 128), E1, 128 * t, XQ, 0, 128) for t in range(4)]
+    t_tk[0] = [A([t_tkm[t]], T["tk%d" % t][:, 0:64], pd(t, 0, 64), scale=0.25) for t in range(4)]
+    t_hs = A([], T.hs[:], T.hz[:, 0:512])
+    t_diag = V([t_c16, t_q], vec.tensor_scalar, T.diag[:], T.c16[:], T.qc[:], None, ALU.is_equal)
+    t_x1 = V([lx1], vec.quantize_mx, T.xq[:, 128:256], T.xqs[:, 128:256], T.xt[:, 512:1024])
+    cst, t_maps = {}, {}
+
+    def make_mk():
+        t_m = V([t_iq], vec.tensor_scalar, T.mk[:], T.iq[:], T.qc[:], -2000.0, ALU.is_equal, ALU.mult)
+        t_qm = V([t_q], vec.tensor_scalar, T.qm[:], T.qc[:], 2000.0, None, ALU.add)
+        t_m1 = V([t_m], vec.tensor_scalar, T.mk[:, 65:260:65], T.iq[:, 65:260:65], 0.0, 100000.0, ALU.mult, ALU.add)
+        t_m = V([t_m, t_qm], vec.tensor_scalar, T.mk[:, 64:260:65], T.iq[:, 64:260:65], -1.0, T.qm[:], ALU.mult, ALU.add)
+        cst["mk"] = [t_m1, t_m]
+
+    def make_ml(b):
+        t_maps[b] = A([cst["base"]], T["ml%d" % b][:, 64:320], T.base[:])
+
+    def squares(eq, n, row, wr, deps):
+        return [A(deps, T[eq][:, n * k:n * k + 64], row, ACTF.Square, bias=T[wr][:, 16 * k + 15:16 * k + 16], scale=64.0)
+                for k in range(4)]
+
+    for b in range(R):
+        W, PJ, TR = ("win%d" % b, "wins%d" % b), ("pj%d" % b, "pjs%d" % b), ("tr%d" % b, "trs%d" % b)
+        wb, wa, ub, ua, jl, ll = [T["%s%d" % (n, b)] for n in ("wb", "wa", "ub", "ua", "jl", "ll")]
+        ml, rb, wcb, wca = [T["%s%d" % (n, b)] for n in ("ml", "rb", "wcb", "wca")]
+        dst = T.cores[rank ^ (1 << b)]
+        rid, pid, _s = topo.addr(dst)
+        mask = topo.mask(core, dst)
+        neng = len(topo.engines(core, dst))
+
+        t_s = [mx(t_tab + t_tr[2 * b + h], T.ps[:, 512 * h:512 * h + 256], TR, 128 * h, W, 0, 256) for h in range(2)]
+        t_u = [mx([t_e1[t]] + (t_cm if b else t_tk[0]), pd(t, 0, 256), E1, 128 * t, W, 0, 256) for t in range(4)]
+        if b == 0:
+            make_rep(1)
+            make_rep(2)
+            t_dgn = V([t_c16, t_q], vec.tensor_scalar, T.diagn[:], T.c16[:, 0:32], T.qc[:], -64.0, ALU.is_equal, ALU.mult)
+        elif b == 1:
+            tr_codes(2, 0, t_x1)
+            tr_codes(2, 1, t_x1)
+        else:
+            t_wq = V([lw], vec.quantize_mx, T.wq[:], T.wqs[:], T.wt[:])
+        t_w, t_sc = [], []
+        for h in range(2):
+            pm = T["pm%d" % h]
+            t = V([t_s[h], t_neg], vec.tensor_tensor_scan, pm[:], T.ps[:, 512 * h:512 * h + 256], T.neg[:], -1.0e29, ALU.max, ALU.max)
+            t_sc.append(t)
+            t_w.append(A([t], T["sg%d" % h][:], pm[:], ACTF.Sign, bias=pm[:, 255:256], scale=-1.0, accum_out=wcb[:, h:h + 1]))
+        need("G", t_w)
+        g.remote_dma(wca[:], wcb[:], T.sem["rl%d" % b], T.sem.loc, pid, rid, mask)
+        if b == 0:
+            t_rs = V([t_c16], vec.tensor_scalar, T.rs[:], T.c16[:], 0.0, None, ALU.is_gt)
+        t = V([t_w[0], t_dgn], vec.tensor_scalar, T.tinb[:, 0:32], T.diagn[:], wcb[:, 0:1], None, ALU.mult)
+        t_dk = [V([t_u[0]], vec.tensor_scalar, T.dk0[:], pd(0, 0, 256), 0.75, None, ALU.mult)]
+        for i in (1, 2, 3):
+            t_dk.append(A([t_u[i]], T["dk%d" % i][:], pd(i, 0, 256), scale=0.75))
+        t1 = V([t_w[1]], vec.tensor_scalar, T.tinb[:, 32:64], T.diagn[:], wcb[:, 1:2], None, ALU.mult)
+        t = V([t, t1], vec.transpose, T.toutb[:], T.tinb[:])
+        t_wr = V([t, t_rs], vec.tensor_tensor_scan, T.wrb[:], T.rs[:, 0:64], T.toutb[:], 0.0, ALU.mult, ALU.add)
+        t_wb = V([t_wr], vec.tensor_scalar, wb[:], T.wrb[:, 15:64:16], -0.015625, None, ALU.mult)
+
+        t_cs = [V([t_wb, t_dk[t], t_hs] + t_tk[b], vec.tensor_tensor, T.hs[:, t:256:4], T["dk%d" % t][:].indirect(wb[:]),
+                  T["tk%d" % t][:, NT * b:NT * b + NT], ALU.add) for t in range(4)]
+        t_n = V(t_cs, vec.quantize_mx, T[W[0]][:, 320:448], T[W[1]][:, 320:448], T.hs[:])
+        need("G", [t_n])
+        g.remote_dma(w8(W[0], 256, 320), w8(W[0], 320, 384), T.sem["rd%d" % b], T.sem.loc, pid, rid, mask)
+        g.remote_dma(T[W[1]][:, 256:320], T[W[1]][:, 320:384], T.sem["rd%d" % b], T.sem.loc, pid, rid, mask)
+
+        t_rb = A([t_wb, t_row], rb[:], T.row[:, 0:256].indirect(wb[:]))
+        ts = [A([t_wr], T.eqb[:, 64:260:65], T.wrb[:, 15:64:16], scale=-0.015625)]
+        ts += squares("eqb", 65, rb[:], "wrb", [t_wr, t_rb])
+        if b == 0:
+            t_hm = A([], T.hm[:], T.hz[:, 0:512])
+            cst["base"] = V([t_diag, t_row], vec.tensor_tensor, T.base[:], T.diag[:], T.row[:, 0:256], ALU.mult)
+            make_mk()
+            make_pj(0)
+            cst["step"] = V([t_row], vec.tensor_scalar, T.step[:], T.row[:, 0:80], 64.0, 1.0, ALU.is_lt, ALU.add)
+            t_tkm = [mx([t_x1, t_e1[i]] + t_sc, px(i, 0, 128), E1, 128 * i, XQ, 128, 128) for i in range(4)]
+            t_tk[1] = t_tk[2] = [A([t_tkm[t]], T["tk%d" % t][:, 64:192], px(t, 0, 128), scale=0.25) for t in range(4)]
+            make_ml(0)
+        arr_l = ("rl%d" % b, neng, {})
+        ta = [A([arr_l, t_dgn], T.tina[:, 32 * h:32 * h + 32], T.diagn[:], scale=wca[:, h:h + 1]) for h in range(2)]
+
+        t3 = V([t_row, t_diag], vec.tensor_tensor, T.t3[:], T.diag[:].indirect(wb[:]), T.row[:, 320:384], ALU.mult)
+        t = V(ta, vec.transpose, T.touta[:], T.tina[:])
+        t_d = V(ts + cst["mk"], vec.tensor_tensor_scan, T.dsb[:], T.mk[:], T.eqb[:], 100000.0, ALU.add, ALU.min)
+        t_wr = V([t], vec.tensor_tensor_scan, T.wra[:], T.rs[:, 0:64], T.touta[:], 0.0, ALU.mult, ALU.add)
+        tj = squares("eqj", 64, rb[:], "wra", [t_wr, t_rb])
+        t_ub = V([t_d], vec.tensor_scalar, ub[:], T.dsb[:, 64:260:65], 64.0, None, ALU.add)
+        t_wa = V([t_wr], vec.tensor_scalar, wa[:], T.wra[:, 15:64:16], -0.015625, None, ALU.mult)
+        t_ra = A([t_wa, t_row], T.ra[:], T.row[:, 0:256].indirect(wa[:]))
+        ts = [A([t_wr], T.eqa[:, 64:260:65], T.wra[:, 15:64:16], scale=-0.015625)]
+        ts += squares("eqa", 65, T.ra[:], "wra", [t_wr, t_ra])
+        t_vd = V([t_wa], vec.tensor_tensor, T.vd[:], T.diag[:].indirect(wa[:]), T.row[:, 256:320], ALU.mult)
+        t_ml = V([t3, t_ub, t_maps[b]], vec.tensor_copy, ml[:].indirect(ub[:]), T.t3[:])
+        t_j = V(tj + t_jm, vec.tensor_tensor_scan, T.dsj[:], T.jmk[:], T.eqj[:], 100000.0, ALU.add, ALU.min)
+        t_jl = V([t_j], vec.tensor_scalar, jl[:], T.dsj[:, 63:256:64], 63.0, 64.0, ALU.add, ALU.min)
+        t_p = pick(PJ, 64, 128, W, 320, 448, jl[:], [t_jl, t_pj[b]])
+        if b + 1 < R:
+            for h in range(2):
+                tr_scales(b + 1, h, t_x1)
+            make_ml(b + 1)
+        arr_d = ("rd%d" % b, 2 * neng, {})
+        for i in range(4):
+            mx([arr_d] + t_dk, pd(i, 0, 128), E1, 128 * i, W, 192, 128, True, False)
+        t_d = [mx(t_p, pd(i, 0, 128), E1, 128 * i, PJ, 0, 128, False, True) for i in range(4)]
+        t_cm = [A([t_d[i], t_hm], T.hm[:, i:512:8], pd(i, 64, 128), scale=0.5) for i in range(4)]
+        t = V(ts, vec.tensor_tensor_scan, T.dsa[:], T.mk[:], T.eqa[:], 100000.0, ALU.add, ALU.min)
+        t_va = V([t_jl, t_vd, cst["step"]], vec.tensor_tensor, T.va[:], T.step[:].indirect(jl[:]), T.vd[:], ALU.mult)
+        t_ua = V([t], vec.tensor_scalar, ua[:], T.dsa[:, 64:260:65], 64.0, None, ALU.add)
+        t = V([t_ua, t_va, t_ml], vec.tensor_copy, ml[:].indirect(ua[:]), T.va[:])
+        t = V([t], vec.tensor_tensor_scan, T.ls[:], T.rs[:], ml[:, 64:320], 0.0, ALU.mult, ALU.add)
+        if b == 0:
+            tr_codes(1, 0, t_x1)
+        t_ll = V([t], vec.tensor_copy, ll[:], T.ls[:, 15:256:16])
+        t_m = V(t_cm, vec.quantize_mx, T[W[0]][:, 512:640], T[W[1]][:, 512:640], T.hm[:])
+        dma("S", [t_rb], "st", T.ch[b:b + 1, 0:NT], rb[0:1, :])
+        if b + 1 < R:
+            t_tab = pick(("win%d" % (b + 1), "wins%d" % (b + 1)), 0, 256, W, 0, 640, ll[:], [t_m, t_ll])
+            make_pj(b + 1)
+            if b == 0:
+                tr_codes(1, 1, t_x1)
+
+    K = ("k3", "k3s")
+    t_h = [pick(K, 128 * m, 128 * m + 128, W, 0, 640, ll[:, 8 * m:8 * m + 8], [t_m, t_ll]) for m in range(2)]
+    t_y = [mx([t_wq] + t_h[m], T.ps[:, 512 * m:512 * m + 128], ("wq", "wqs"), 0, K, 128 * m, 128) for m in range(2)]
+    t_ya = A([t_y[0]], T.yt[:, 0:128], T.ps[:, 0:128])
+    dma("A", [t_ya], "st", T.y[:, 0:128], T.yt[:, 0:128])
+    t_yv = V([t_y[1]], vec.tensor_copy, T.yt[:, 128:256], T.ps[:, 512:640])
+    for m in range(2):
+        dma("S", t_h[m][0:1], "st", T.oc[:, 512 * m:512 * m + 512], w8("k3", 128 * m, 128 * m + 128))
+    for k in range(4):
+        dma("AASS"[k], t_h[1][1:2], "st", T.osc[4 * k:4 * k + 4, :], T.k3s[32 * k:32 * k + 4, :])
+    dma("S", [t_yv], "st", T.y[:, 128:256], T.yt[:, 128:256])
+    g.sync.wait_ge(T.sem.st, 16 * (R + 8))
+    g.wait_ge(T.sem.loc, 3 * R * neng)

@@ -3,276 +3,313 @@ from concourse.mybir import dt, AluOpType, ActivationFunctionType
 ALU = AluOpType
 ACTF = ActivationFunctionType
 R = 3
-NT = 64
+TKQ = "AAAA"
+DKQ = "VAAA"
+ODQ = "AAAA"
+CJQ = "AAAA"
+GQ = "V"
+YQ = "AVAV"
+OQ = "SSAASS"
+S = 512.0
+DROP = 321.0 * S
+HUGE = 1.0e6
+ALL = (0, 128)
 
 X4 = "float8_e4m3fn_x4"
-SCRATCH = {"ps": ("psum", [128, 1024], "float32"), "pd": ("psum", [128, 2048], "float32"), "pe": ("psum", [128, 1024], "float32"),
-           "pidx": ("sbuf", [128, 1], "int32"), "pand": ("sbuf", [128, 1], "int32")}
-for _n, _w in (("xt", 1024), ("kt", 1024), ("wt", 512), ("z1", 516), ("hs", 512), ("hm", 512), ("hz", 516), ("sg0", 256), ("sg1", 256)):
+SCRATCH = {"pa": ("psum", [128, 2048], "float32"), "pb": ("psum", [128, 2048], "float32"),
+           "pidx": ("sbuf", [128, 1], "int32"), "pand": ("sbuf", [128, 1], "int32"), "rep": ("sbuf", [128, 8], "uint16")}
+for _n, _w in (("xt", 512), ("xr", 1024), ("kt", 1024), ("wt", 512), ("z", 516), ("h", 768), ("sg", 256)):
     SCRATCH[_n] = ("sbuf", [128, _w], "bfloat16")
-for _n, _w in (("qc", 1), ("qm", 1), ("repi", 16), ("c16", 256), ("row", 384), ("iq", 260), ("mk", 260), ("diag", 256),
-               ("diagn", 32), ("rs", 256), ("base", 256), ("neg", 256), ("jmk", 256), ("step", 80), ("pm0", 256), ("pm1", 256),
-               ("tinb", 64), ("tina", 64), ("toutb", 64), ("touta", 64), ("wrb", 64), ("wra", 64), ("eqb", 260), ("eqa", 260),
-               ("eqj", 256), ("dsb", 260), ("dsa", 260), ("dsj", 256), ("ra", 64), ("t3", 64), ("va", 64), ("vd", 64),
-               ("ls", 256), ("yt", 256), ("dk0", 256), ("dk1", 256), ("dk2", 256), ("dk3", 256),
-               ("tk0", 192), ("tk1", 192), ("tk2", 192), ("tk3", 192)):
+for _n, _w in (("qc", 1), ("qm", 1), ("adj", 1), ("c16", 256), ("row", 448), ("iq", 260), ("mk", 260), ("fm", 256), ("vf", 64),
+               ("pm", 256), ("wc", 1), ("repi", 8), ("eqb", 260), ("dsb", 260), ("eqa", 260), ("dsa", 260), ("ra", 64),
+               ("gr", 64), ("gs", 64), ("va", 64), ("ls", 256), ("yw", 512), ("yt", 256)):
     SCRATCH[_n] = ("sbuf", [128, _w], "float32")
-for _n, _w in (("e1", 512), ("xq", 256), ("wq", 128), ("k3", 256)):
+for _t in range(4):
+    for _n, _w in (("dk", 256), ("tk", 192), ("od", 65), ("cj", 64)):
+        SCRATCH["%s%d" % (_n, _t)] = ("sbuf", [128, _w], "float32")
+for _n, _w in (("e", 512), ("xq", 256), ("tr", 384), ("wq", 128), ("win0", 576), ("win1", 576), ("win2", 576), ("win3", 256)):
     SCRATCH[_n] = ("sbuf", [128, _w], X4)
     SCRATCH[_n + "s"] = ("sbuf", [128, _w], "uint8")
 for _b in range(R):
-    for _n, _w in (("win", 640), ("pj", 128), ("tr", 256)):
-        SCRATCH["%s%d" % (_n, _b)] = ("sbuf", [128, _w], X4)
-        SCRATCH["%ss%d" % (_n, _b)] = ("sbuf", [128, _w], "uint8")
-    for _n, _w in (("rep", 16), ("wb", 4), ("wa", 4), ("ub", 4), ("ua", 4), ("jl", 4), ("ll", 16)):
+    for _n, _w in (("wb", 4), ("wa", 4), ("ub", 4), ("ua", 4), ("jl", 4), ("ll", 16)):
         SCRATCH["%s%d" % (_n, _b)] = ("sbuf", [128, _w], "uint16")
-    for _n, _w in (("ml", 320), ("rb", 64), ("wcb", 2), ("wca", 2)):
+    for _n, _w in (("ml", 320), ("rb", 64)):
         SCRATCH["%s%d" % (_n, _b)] = ("sbuf", [128, _w], "float32")
 
-SEMAPHORES = ["cv", "ca", "cp", "cg", "lx0", "lx1", "lk", "lw", "st", "loc"]
+SEMAPHORES = ["cV", "cA", "cP", "cG", "lx0", "lx1", "lr1", "lr2", "lk", "lw", "st", "loc"]
 for _b in range(R):
-    SEMAPHORES += ["rl%d" % _b, "rd%d" % _b]
+    SEMAPHORES += ["rl%d" % _b, "rd%d" % _b, "lm%d" % _b]
+
+ORDER = """repi lx01 pidx z0 lk lx10 z1 lr10 lr11 c16 lr12 iq lr13 h0 pand qc qx0 lr14 row lr20 lr21 rep e3 tk03 e2 t0s eqb0 t0c lr22 lr23 qk adj
+e1 lr24 ml1 tk02 qx1 e0 eqa0 qm sc0 tc02 tk01 pm0 mk0 fm0 tc03 tc01 tk00 sg0 la01 la02 la00 la03 du01 du02 mk2 tc00 ml0 lb03 lb02 lb01 du03
+du00 sl0 mk1 dc01 dc02 dc00 dc03 sh02 wf0 rb0 b0q2 b0q1 sh01 b0q0 al0 sh00 sh03 sq0 b0q3 qr2 b0s ou00 fm1 ou03 ou02 sc_0 ou01 od00 od02 od01
+b0u ra0 qr1 mb0 af0 ss_0 gr0 od03 a0q3 a0q1 a0q2 a0q0 ad0 tk13 tk10 vf0 gs0 jl0 a0s au02 au00 va0 lw a0u cj00 cj02 ma0 mh02 cj03 cj01 tc10
+au03 mh00 mh03 au01 mh01 ls0 ml2 tk12 tk11 tc12 tc13 tc11 mq0 ll0 tp0s tp0c sc1 pm1 du10 dc10 du12 du11 du13 qw sg1 la11 la10 la12 la13 lb12
+lb13 lb11 dc11 dc12 dc13 wf1 sh12 sl1 rb1 b1q0 b1q2 b1q1 sh10 sh13 sh11 sq1 b1q3 sc_1 ss_1 b1s ad1 al1 ra1 b1u af1 mb1 ou12 gr1 vf1 ou10 ou13
+ou11 a1q2 a1q3 a1q1 a1q0 od11 od10 a1s gs1 od12 od13 au10 va1 jl1 a1u cj10 cj13 cj11 cj12 au13 au11 au12 ma1 ch0 mh10 ls1 mh11 mh13 mh12 ll1
+mq1 tp1s tp1c sc2 du20 du23 pm2 sg2 dc20 du21 dc23 la23 du22 dc22 dc21 la20 la22 la21 lb22 lb21 lb23 sl2 wf2 sh20 sh23 sh21 sh22 sq2 ou23 ou22
+sc_2 ou21 ou20 ss_2 rb2 b2q1 b2q2 b2q3 al2 ad2 au23 au22 b2q0 b2s b2u ra2 af2 od23 ch1 a2q1 a2q0 a2q2 od21 a2q3 mb2 od20 au21 au20 ch2 y0 gr2
+vf2 gs2 a2s jl2 od22 va2 cj22 cj23 cj20 y1 a2u ma2 cj21 mh23 mh22 ls2 mh20 mh21 yc0 ll2 mq2 tp2s yc1 y2 tp2c oc os2 yc2 yp1 yp0 os0 oy0 oy1
+os3 os1"""
+
+
+def X(name, a=0, b=None, step=1, part=ALL, cast=None, off=None):
+    return ("view", name, a, SCRATCH[name][1][1] if b is None else b, step, part, cast, off)
+
+
+def is_view(x):
+    return isinstance(x, tuple) and len(x) == 8 and x[0] == "view"
+
+
+def meets(x, y):
+    if x[1] != y[1] or x[5][1] <= y[5][0] or y[5][1] <= x[5][0] or x[3] <= y[2] or y[3] <= x[2]:
+        return False
+    return x[4] == 1 and y[4] == 1 or bool(set(range(x[2], x[3], x[4])) & set(range(y[2], y[3], y[4])))
+
+
+def same_bank(x, y):
+    return x[1] == y[1] and SCRATCH[x[1]][0] == "psum" and x[2] // 512 == y[2] // 512
+
+
+def plan(g, T):
+    ops = []
+    vec, act, ten = g.vector, g.scalar, g.tensor
+
+    def op(name, q, fn, args, kw, outs, sem=None, kind="c"):
+        views = [a for a in list(args) + list(kw.values()) if is_view(a)]
+        reads = [a for a in views if not any(a is o for o in outs)] + [a[7] for a in views if a[7] is not None]
+        ops.append({"name": name, "q": q, "fn": fn, "args": args, "kw": kw, "rd": reads, "wr": list(outs), "sem": sem, "kind": kind})
+
+    def V(name, fn, out, *args):
+        op(name, "V", fn, (out,) + args, {}, [out])
+
+    def G(name, fn, out, *args, **kw):
+        op(name, "G", fn, (out,) + args, kw, [out])
+
+    def A(name, out, in_, func=ACTF.Copy, **kw):
+        op(name, "A", act.activation, (out, in_, func), kw, [out] + ([kw["accum_out"]] if "accum_out" in kw else []))
+
+    def iota(name, out, pattern):
+        G(name, g.iota, out, pattern, 0, 0, allow_small_or_imprecise_dtypes=True)
+
+    def quant(name, buf, a, b, tile):
+        c, s = X(buf, a, b), X(buf + "s", a, b)
+        op(name, "V", vec.quantize_mx, (c, s, tile), {}, [c, s])
+
+    def mx(name, out, st, a, mv, c, n):
+        op(name, "P", ten.matmul_mx, (out, X(st, a, a + 128), X(st + "s", a, a + 128), X(mv, c, c + n), X(mv + "s", c, c + n), True, True), {}, [out])
+
+    def pick(name, out, a, b, win, n, off):
+        V(name + "c", vec.tensor_copy, X(out, a, b, cast=dt.uint32), X(win, 0, n, cast=dt.uint32, off=off))
+        A(name + "s", X(out + "s", a, b), X(win + "s", 0, n, off=off))
+
+    def dma(name, q, sem, out, in_):
+        op(name, q, (g.sync if q == "S" else act).dma_start, (out, in_), {}, [out] if is_view(out) else [], sem, "d")
+
+    def send(name, sem, out, in_):
+        ops.append({"name": name, "q": "G", "args": (out, in_), "kw": {}, "rd": [in_], "wr": [], "sem": sem, "kind": "r"})
+
+    def landed(name, sem, outs, sends):
+        ops.append({"name": name, "q": None, "rd": [], "wr": outs, "sem": sem, "kind": "a", "sends": sends})
+
+    def copy(name, q, out, in_, f=1.0):
+        if q == "A":
+            A(name, out, in_, **({} if f == 1.0 else {"scale": f}))
+        elif f == 1.0:
+            V(name, vec.tensor_copy, out, in_)
+        else:
+            V(name, vec.tensor_scalar, out, in_, f, None, ALU.mult)
+
+    def fold(name, out, in_, n):
+        V(name, vec.tensor_tensor_scan, out, X("fm", 0, n), in_, 0.0, ALU.add, ALU.min)
+
+    def places(name, eq, ds, row, out):
+        for k in range(4):
+            n = 16 * k + 16
+            A("%sq%d" % (name, k), X(eq, 65 * k, 65 * k + n), X(row, 0, n), ACTF.Square, bias=X(eq, 65 * k + 64, 65 * k + 65), scale=-S)
+        V(name + "s", vec.tensor_tensor_scan, X(ds), X("mk"), X(eq), HUGE, ALU.add, ALU.min)
+        V(name + "u", vec.tensor_scalar, X(out), X(ds, 64, 260, 65), 1.0 / S, 64.0, ALU.mult, ALU.add)
+
+    def bank(buf, t, a, b):
+        return X(buf, 512 * t + a, 512 * t + b)
+
+    dma("lx01", "S", "lx0", X("h", 0, 256), T.x[:, 0:256])
+    dma("lk", "A", "lk", X("kt"), T.kb[:])
+    dma("lx10", "S", "lx1", X("xt"), T.x[:, 256:768])
+    for b in (1, 2):
+        for i in range(5):
+            a, c = max(128 * i - 64, 0), min(128 * i + 64, 512)
+            s = 256 * b + max(64 * i - 64, 0)
+            dma("lr%d%d" % (b, i), "S", "lr%d" % b, X("xr", 512 * b - 512 + a, 512 * b - 512 + c), T.x[:, s:s + c - a])
+    dma("lw", "S", "lw", X("wt"), T.w[:])
+
+    V("z0", vec.memset, X("z"), 0.0)
+    G("pidx", g.iota, X("pidx"), [[0, 1]], 0, 1)
+    G("z1", g.affine_select, X("z", 3, 515, 4), X("z", 3, 515, 4), [[-1, 128]], ALU.not_equal, 0.5, 0, 1)
+    V("h0", vec.memset, X("h", 256, 512), 0.0)
+    for t in range(4):
+        quant("e%d" % t, "e", 128 * t, 128 * t + 128, X("z", 3 - t, 515 - t))
+    iota("c16", X("c16"), [[0, 16], [1, 16]])
+    quant("qx0", "xq", 0, 128, X("h", 0, 512))
+    quant("qk", "win0", 0, 256, X("kt"))
+    V("pand", vec.tensor_scalar, X("pand"), X("pidx"), 15, None, ALU.bitwise_and)
+    V("qc", vec.tensor_copy, X("qc"), X("pand"))
+    iota("repi", X("repi"), [[16, 4], [0, 2]])
+    V("rep", vec.tensor_scalar, X("rep"), X("repi"), X("qc"), None, ALU.add)
+    pick("t0", "tr", 0, 128, "xq", 128, X("rep"))
+    V("adj", vec.tensor_scalar, X("adj"), X("qc"), -1000.0, 15000.0, ALU.mult, ALU.add)
+    V("fm0", vec.tensor_scalar, X("fm"), X("c16"), X("qc"), 101000.0, ALU.is_equal, ALU.mult)
+    A("fm1", X("fm"), X("fm"), bias=-1000.0)
+    iota("iq", X("iq"), [[-16, 4], [1, 65]])
+    iota("row", X("row"), [[1, 448]])
+    V("mk0", vec.tensor_scalar, X("mk"), X("iq"), X("qc"), -DROP, ALU.is_equal, ALU.mult)
+    V("qm", vec.tensor_scalar, X("qm"), X("qc"), S, DROP, ALU.mult, ALU.add)
+    V("mk1", vec.tensor_scalar, X("mk", 65, 260, 65), X("iq", 65, 260, 65), 0.0, HUGE, ALU.mult, ALU.add)
+    V("mk2", vec.tensor_scalar, X("mk", 64, 260, 65), X("iq", 64, 260, 65), -S, X("qm"), ALU.mult, ALU.add)
+    A("eqb0", X("eqb", 0, 195), X("h", 256, 451))
+    A("eqa0", X("eqa", 0, 195), X("h", 256, 451))
+    for b in range(R):
+        dma("ml%d" % b, "S", "lm%d" % b, X("ml%d" % b, 64, 320), X("row", 0, 256))
+    quant("qx1", "xq", 128, 256, X("xt"))
+    quant("qr1", "tr", 128, 256, X("xr", 0, 512))
+    quant("qr2", "tr", 256, 384, X("xr", 512, 1024))
+    quant("qw", "wq", 0, 128, X("wt"))
+
+    for b in range(R):
+        W, N, n = "win%d" % b, "win%d" % (b + 1), str(b)
+        wb, wa, ub, ua, jl, ll, ml, rb = [nm + n for nm in ("wb", "wa", "ub", "ua", "jl", "ll", "ml", "rb")]
+
+        mx("sc" + n, bank("pb", 0, 0, 256), "tr", 128 * b, W, 0, 256)
+        V("pm" + n, vec.tensor_tensor_scan, X("pm"), X("h", 256, 512), bank("pb", 0, 0, 256), -1.0e29, ALU.add, ALU.max)
+        for t in range(4):
+            if b < 2:
+                mx("tk%d%d" % (b, t), bank("pa", t, 0, 128), "e", 128 * t, "xq", 128 * b, 128)
+                copy("tc%d%d" % (b, t), TKQ[t], X("tk%d" % t, 64 * b, 128 * b + 64), bank("pa", t, 0, 64 * b + 64), 0.5)
+            mx("du%d%d" % (b, t), bank("pa", t, 0, 256), "e", 128 * t, W, 0, 256)
+            copy("dc%d%d" % (b, t), DKQ[t], X("dk%d" % t), bank("pa", t, 0, 256), 1.5)
+        A("sg" + n, X("sg"), X("pm"), ACTF.Sign, bias=X("pm", 255, 256), scale=-1.0, accum_out=X("wc"))
+        for k in range(4):
+            V("la%d%d" % (b, k), vec.tensor_copy, X(wb, k, k + 1, part=(0, 32)), X("wc", part=(32 * k, 32 * k + 32)))
+        for k in range(1, 4):
+            V("lb%d%d" % (b, k), vec.tensor_copy, X(wb, part=(32 * k, 32 * k + 32)), X(wb, part=(0, 32)))
+        send("sl" + n, "rl" + n, X(wa), X(wb))
+
+        for t in range(4):
+            V("sh%d%d" % (b, t), vec.tensor_tensor, X("h", 512 + t, 768, 4), X("dk%d" % t, off=X(wb)), X("tk%d" % t, 64 * b, 64 * b + 64), ALU.add)
+        quant("sq" + n, W, 256, 384, X("h", 256, 768))
+        send("sc_" + n, "rd" + n, X(W, 384, 448, cast=dt.uint8), X(W, 320, 384, cast=dt.uint8))
+        send("ss_" + n, "rd" + n, X(W + "s", 384, 448), X(W + "s", 320, 384))
+
+        A("rb" + n, X(rb), X("row", 0, 256, off=X(wb)))
+        V("wf" + n, vec.tensor_scalar, X("eqb", 64, 260, 65), X(wb), S, None, ALU.mult)
+        places("b" + n, "eqb", "dsb", rb, ub)
+        V("mb" + n, vec.tensor_copy, X(ml, off=X(ub)), X("row", 320, 384))
+        dma("ch" + n, "S", "st", T.ch[b:b + 1, 0:64], X(rb, part=(0, 1)))
+
+        landed("al" + n, "rl" + n, [X(wa)], ["sl" + n])
+        copy("gr" + n, GQ, X("gr"), X(ml, 64, 320, off=X(wa)))
+        fold("gs" + n, X("gs"), X("gr"), 64)
+        V("jl" + n, vec.tensor_scalar, X(jl), X("gs", 15, 64, 16), X("adj"), -319.0, ALU.add, ALU.add)
+        for t in range(4):
+            mx("ou%d%d" % (b, t), bank("pa", t, 0, 128), "e", 128 * t, W, 256, 128)
+            copy("od%d%d" % (b, t), ODQ[t], X("od%d" % t), bank("pa", t, 63, 128))
+            copy("cj%d%d" % (b, t), CJQ[t], X("cj%d" % t), X("od%d" % t, off=X(jl)))
+        V("vf" + n, vec.tensor_scalar, X("vf"), X(ml, 64, 320, off=X(wa)), 320.0, 64.0, ALU.is_ge, ALU.mult)
+        V("va" + n, vec.tensor_tensor, X("va"), X("vf"), X("row", 384, 448), ALU.add)
+        A("ra" + n, X("ra"), X("row", 0, 256, off=X(wa)))
+        V("af" + n, vec.tensor_scalar, X("eqa", 64, 260, 65), X(wa), S, None, ALU.mult)
+        places("a" + n, "eqa", "dsa", "ra", ua)
+        V("ma" + n, vec.tensor_copy, X(ml, off=X(ua)), X("va"))
+        fold("ls" + n, X("ls"), X(ml, 64, 320), 256)
+        V("ll" + n, vec.tensor_scalar, X(ll), X("ls", 15, 256, 16), X("adj"), None, ALU.add)
+
+        landed("ad" + n, "rd" + n, [X(W, 384, 448), X(W + "s", 384, 448)], ["sc_" + n, "ss_" + n])
+        for t in range(4):
+            mx("au%d%d" % (b, t), bank("pb", t, 0, 128), "e", 128 * t, W, 320, 128)
+            V("mh%d%d" % (b, t), vec.tensor_tensor, X("h", t, 256, 4), bank("pb", t, 64, 128), X("cj%d" % t), ALU.add)
+        quant("mq" + n, W, 448, 576, X("h", 0, 512))
+        pick("tp" + n, N, 0, 256, W, 512, X(ll))
+
+    for i, (a, c) in enumerate(((0, 320), (320, 448), (448, 576))):
+        mx("y%d" % i, bank("pa", i, 0, c - a), "wq", 0, W, a, c - a)
+        copy("yc%d" % i, YQ[i], X("yw", a, min(c, 512)), bank("pa", i, 0, min(c, 512) - a))
+    for m in range(2):
+        copy("yp%d" % m, YQ[2 + m], X("yt", 128 * m, 128 * m + 128), X("yw", off=X(ll, 8 * m, 8 * m + 8)))
+        dma("oy%d" % m, OQ[m], "st", T.y[:, 128 * m:128 * m + 128], X("yt", 128 * m, 128 * m + 128))
+    dma("oc", "S", "st", T.oc[:], X(N, cast=dt.uint8))
+    for k in range(4):
+        dma("os%d" % k, OQ[2 + k], "st", T.osc[4 * k:4 * k + 4, :], X(N + "s", part=(32 * k, 32 * k + 4)))
+
+    for i, o in enumerate(ops):
+        o["deps"] = []
+        for e in ops[:i]:
+            if o["q"] == "P" and e["q"] == "P":
+                continue
+            if (any(meets(x, y) for x in o["rd"] + o["wr"] for y in e["wr"]) or any(meets(x, y) for x in o["wr"] for y in e["rd"])
+                    or o["q"] != e["q"] and any(same_bank(x, y) for x in o["rd"] + o["wr"] for y in e["rd"] + e["wr"])):
+                o["deps"].append(e["name"])
+    return ops
 
 
 def rank_program(g, core, T, topo):
     rank = T.rank_of(core)
     if rank is None:
         return
-    queues = {"V": (g.vector, "cv"), "A": (g.scalar, "ca"), "P": (g.tensor, "cp"), "G": (g, "cg"), "S": (g.sync, None)}
-    issued = {"cv": 0, "ca": 0, "cp": 0, "cg": 0}
+    ops = plan(g, T)
+    by_name = {o["name"]: o for o in ops}
+    order = ORDER.split() if ORDER else [o["name"] for o in ops]
+    queues = {"V": g.vector, "A": g.scalar, "P": g.tensor, "G": g, "S": g.sync}
     known = {q: {} for q in queues}
-
-    def need(q, deps):
-        for sem, val, through in deps:
-            if known[q].get(sem, 0) < val:
-                queues[q][0].wait_ge(T.sem[sem], val)
-                known[q][sem] = val
-                for s, v in through.items():
-                    known[q][s] = max(known[q].get(s, 0), v)
-
-    def do(q, deps, fn, *args, **kw):
-        need(q, deps)
-        sem = queues[q][1]
-        issued[sem] += 1
-        fn(*args, **kw).then_inc(T.sem[sem], 1)
-        return (sem, issued[sem], dict(known[q]))
-
-    def dma(q, deps, sem, out, in_):
-        need(q, deps)
-        queues[q][0].dma_start(out, in_).then_inc(T.sem[sem], 16)
-        return (sem, 16, dict(known[q]))
-
-    vec, act, ten = g.vector, g.scalar, g.tensor
-
-    def V(deps, fn, *args, **kw):
-        return do("V", deps, fn, *args, **kw)
-
-    def A(deps, out, in_, func=ACTF.Copy, **kw):
-        return do("A", deps, act.activation, out, in_, func, **kw)
-
-    def mx(deps, bank, st, a, mv, c, n, start=True, stop=True):
-        return do("P", deps, ten.matmul_mx, bank, T[st[0]][:, a:a + 128], T[st[1]][:, a:a + 128],
-                  T[mv[0]][:, c:c + n], T[mv[1]][:, c:c + n], start, stop)
-
-    def pd(t, a, b):
-        return T.pd[:, 512 * t + a:512 * t + b]
-
-    def px(t, a, b):
-        return (T.ps, T.pe)[t // 2][:, 512 * (t % 2) + a:512 * (t % 2) + b]
-
-    def w8(name, a, b):
-        return T[name][:, a:b].bitcast(dt.uint8)
-
-    def w32(name, a, b):
-        return T[name][:, a:b].bitcast(dt.uint32)
-
-    def pick(out, a, b, win, c, d, off, deps):
-        tc = V(deps, vec.tensor_copy, w32(out[0], a, b), w32(win[0], c, d).indirect(off))
-        ts = A(deps, T[out[1]][:, a:b], T[win[1]][:, c:d].indirect(off))
-        return [tc, ts]
-
-    E1, XQ = ("e1", "e1s"), ("xq", "xqs")
-
-    lx0 = dma("S", [], "lx0", T.xt[:, 0:256], T.x[:, 0:256])
-    lk = dma("A", [], "lk", T.kt[:], T.kb[:])
-    lx1 = dma("S", [], "lx1", T.xt[:, 512:1024], T.x[:, 256:768])
-    lw = dma("S", [], "lw", T.wt[:], T.w[:])
-
-    t_z0 = V([], vec.memset, T.z1[:], 0.0)
-    t_pidx = do("G", [], g.iota, T.pidx[:], [[0, 1]], 0, 1)
-    t_repi = do("G", [], g.iota, T.repi[:], [[32, 2], [0, 4], [16, 2]], 0, 0, allow_small_or_imprecise_dtypes=True)
-    t_z1 = do("G", [t_z0], g.affine_select, T.z1[:, 3:515:4], T.z1[:, 3:515:4], [[-1, 128]], ALU.not_equal, 1.0, 0, 1)
-    t_c16 = do("G", [], g.iota, T.c16[:], [[0, 16], [1, 16]], 0, 0, allow_small_or_imprecise_dtypes=True)
-    t_row = do("G", [], g.iota, T.row[:], [[1, 384]], 0, 0, allow_small_or_imprecise_dtypes=True)
-    t_iq = do("G", [], g.iota, T.iq[:], [[-16, 4], [1, 65]], 0, 0, allow_small_or_imprecise_dtypes=True)
-
-    t_hz = V([], vec.memset, T.hz[:], 0.0)
-    t_xz = A([t_hz], T.xt[:, 256:512], T.hz[:, 0:256])
-    t_and = V([t_pidx], vec.tensor_scalar, T.pand[:], T.pidx[:], 15, None, ALU.bitwise_and)
-    t_q = V([t_and], vec.tensor_copy, T.qc[:], T.pand[:])
-    t_neg = A([t_hz], T.neg[:], T.hz[:, 0:256], ACTF.Copy, bias=-1.0e29)
-    t_jm = [A([t_hz], T.jmk[:], T.hz[:, 0:256], ACTF.Copy, bias=-1.0)]
-    t_jm.append(A(t_jm, T.jmk[:, 0:256:64], T.hz[:, 0:4], ACTF.Copy, bias=100000.0))
-    t_rep, t_pj, t_e1 = {}, {}, []
-
-    def make_rep(b):
-        t_rep[b] = V([t_q, t_repi], vec.tensor_scalar, T["rep%d" % b][:], T.repi[:], T.qc[:], float((0, 128, 192)[b]), ALU.add, ALU.add)
-
-    def make_pj(b):
-        t_pj[b] = V([t_hz], vec.quantize_mx, T["pj%d" % b][:], T["pjs%d" % b][:], T.hz[:, 0:512])
-
-    t_tr = [[] for _ in range(2 * R)]
-    t_tk = {}
-
-    def tr_codes(b, h, dep):
-        t_tr[2 * b + h].append(V([dep, t_rep[b]], vec.tensor_copy, w32("tr%d" % b, 128 * h, 128 * h + 128),
-                                 w32("xq", 0, 256 if b else 128).indirect(T["rep%d" % b][:, 8 * h:8 * h + 8])))
-
-    def tr_scales(b, h, dep):
-        t_tr[2 * b + h].append(A([dep, t_rep[b]], T["trs%d" % b][:, 128 * h:128 * h + 128],
-                                 T.xqs[:, 0:256 if b else 128].indirect(T["rep%d" % b][:, 8 * h:8 * h + 8])))
-
-    make_rep(0)
-    t_x0 = V([lx0, t_xz], vec.quantize_mx, T.xq[:, 0:128], T.xqs[:, 0:128], T.xt[:, 0:512])
-    for i in range(4):
-        t_e1.append(V([t_z1], vec.quantize_mx, T.e1[:, 128 * i:128 * i + 128], T.e1s[:, 128 * i:128 * i + 128], T.z1[:, 3 - i:515 - i]))
-    tr_codes(0, 0, t_x0)
-    for h in range(2):
-        tr_scales(0, h, t_x0)
-    t_tab = [V([lk], vec.quantize_mx, T.win0[:, 0:256], T.wins0[:, 0:256], T.kt[:])]
-    tr_codes(0, 1, t_x0)
-    t_tkm = [mx([t_x0, t_e1[t]], pd(t, 0, 128), E1, 128 * t, XQ, 0, 128) for t in range(4)]
-    t_tk[0] = [A([t_tkm[t]], T["tk%d" % t][:, 0:64], pd(t, 0, 64), scale=0.25) for t in range(4)]
-    t_hs = A([], T.hs[:], T.hz[:, 0:512])
-    t_diag = V([t_c16, t_q], vec.tensor_scalar, T.diag[:], T.c16[:], T.qc[:], None, ALU.is_equal)
-    t_x1 = V([lx1], vec.quantize_mx, T.xq[:, 128:256], T.xqs[:, 128:256], T.xt[:, 512:1024])
-    cst, t_maps = {}, {}
-
-    def make_mk():
-        t_m = V([t_iq], vec.tensor_scalar, T.mk[:], T.iq[:], T.qc[:], -2000.0, ALU.is_equal, ALU.mult)
-        t_qm = V([t_q], vec.tensor_scalar, T.qm[:], T.qc[:], 2000.0, None, ALU.add)
-        t_m1 = V([t_m], vec.tensor_scalar, T.mk[:, 65:260:65], T.iq[:, 65:260:65], 0.0, 100000.0, ALU.mult, ALU.add)
-        t_m = V([t_m, t_qm], vec.tensor_scalar, T.mk[:, 64:260:65], T.iq[:, 64:260:65], -1.0, T.qm[:], ALU.mult, ALU.add)
-        cst["mk"] = [t_m1, t_m]
-
-    def make_ml(b):
-        t_maps[b] = A([cst["base"]], T["ml%d" % b][:, 64:320], T.base[:])
-
-    def squares(eq, n, row, wr, deps):
-        return [A(deps, T[eq][:, n * k:n * k + 64], row, ACTF.Square, bias=T[wr][:, 16 * k + 15:16 * k + 16], scale=64.0)
-                for k in range(4)]
-
+    count, token, total, waited = {}, {}, {}, {}
+    to = []
     for b in range(R):
-        W, PJ, TR = ("win%d" % b, "wins%d" % b), ("pj%d" % b, "pjs%d" % b), ("tr%d" % b, "trs%d" % b)
-        wb, wa, ub, ua, jl, ll = [T["%s%d" % (n, b)] for n in ("wb", "wa", "ub", "ua", "jl", "ll")]
-        ml, rb, wcb, wca = [T["%s%d" % (n, b)] for n in ("ml", "rb", "wcb", "wca")]
         dst = T.cores[rank ^ (1 << b)]
         rid, pid, _s = topo.addr(dst)
-        mask = topo.mask(core, dst)
-        neng = len(topo.engines(core, dst))
+        to.append((pid, rid, topo.mask(core, dst), len(topo.engines(core, dst))))
+    for o in ops:
+        if o["kind"] == "d":
+            total[o["sem"]] = total.get(o["sem"], 0) + 16
+        if o["kind"] == "r":
+            total[o["sem"]] = total.get(o["sem"], 0) + to[int(o["sem"][-1])][3]
+            total["loc"] = total.get("loc", 0) + to[int(o["sem"][-1])][3]
 
-        t_s = [mx(t_tab + t_tr[2 * b + h], T.ps[:, 512 * h:512 * h + 256], TR, 128 * h, W, 0, 256) for h in range(2)]
-        t_u = [mx([t_e1[t]] + (t_cm if b else t_tk[0]), pd(t, 0, 256), E1, 128 * t, W, 0, 256) for t in range(4)]
-        if b == 0:
-            make_rep(1)
-            make_rep(2)
-            t_dgn = V([t_c16, t_q], vec.tensor_scalar, T.diagn[:], T.c16[:, 0:32], T.qc[:], -64.0, ALU.is_equal, ALU.mult)
-        elif b == 1:
-            tr_codes(2, 0, t_x1)
-            tr_codes(2, 1, t_x1)
+    def real(x):
+        if not is_view(x):
+            return x
+        _v, name, a, b, step, part, cast, off = x
+        ap = T[name][slice(None) if part == ALL else slice(part[0], part[1]), slice(a, b) if step == 1 else slice(a, b, step)]
+        if cast is not None:
+            ap = ap.bitcast(cast)
+        return ap if off is None else ap.indirect(real(off))
+
+    for name in order:
+        o = by_name[name]
+        q = o["q"]
+        if q is None:
+            token[name] = (o["sem"], total[o["sem"]], {})
+            continue
+        wants = [token[d] for d in o["deps"]]
+        most = {}
+        for sem, val, through in wants:
+            most[sem] = max(most.get(sem, 0), val)
+        for sem, val in most.items():
+            if known[q].get(sem, 0) < val and not any(w[2].get(sem, 0) >= val for w in wants):
+                queues[q].wait_ge(T.sem[sem], val)
+                waited[sem] = max(waited.get(sem, 0), val)
+        for sem, val, through in wants:
+            for s, v in list(through.items()) + [(sem, val)]:
+                known[q][s] = max(known[q].get(s, 0), v)
+        args, kw = [real(a) for a in o["args"]], {k: real(a) for k, a in o["kw"].items()}
+        if o["kind"] == "r":
+            pid, rid, mask, _n = to[int(o["sem"][-1])]
+            g.remote_dma(args[0], args[1], T.sem[o["sem"]], T.sem.loc, pid, rid, mask)
+        elif o["kind"] == "d":
+            o["fn"](*args).then_inc(T.sem[o["sem"]], 16)
+            token[name] = (o["sem"], total[o["sem"]], dict(known[q]))
         else:
-            t_wq = V([lw], vec.quantize_mx, T.wq[:], T.wqs[:], T.wt[:])
-        t_w, t_sc = [], []
-        for h in range(2):
-            pm = T["pm%d" % h]
-            t = V([t_s[h], t_neg], vec.tensor_tensor_scan, pm[:], T.ps[:, 512 * h:512 * h + 256], T.neg[:], -1.0e29, ALU.max, ALU.max)
-            t_sc.append(t)
-            t_w.append(A([t], T["sg%d" % h][:], pm[:], ACTF.Sign, bias=pm[:, 255:256], scale=-1.0, accum_out=wcb[:, h:h + 1]))
-        need("G", t_w)
-        g.remote_dma(wca[:], wcb[:], T.sem["rl%d" % b], T.sem.loc, pid, rid, mask)
-        if b == 0:
-            t_rs = V([t_c16], vec.tensor_scalar, T.rs[:], T.c16[:], 0.0, None, ALU.is_gt)
-        t = V([t_w[0], t_dgn], vec.tensor_scalar, T.tinb[:, 0:32], T.diagn[:], wcb[:, 0:1], None, ALU.mult)
-        t_dk = [V([t_u[0]], vec.tensor_scalar, T.dk0[:], pd(0, 0, 256), 0.75, None, ALU.mult)]
-        for i in (1, 2, 3):
-            t_dk.append(A([t_u[i]], T["dk%d" % i][:], pd(i, 0, 256), scale=0.75))
-        t1 = V([t_w[1]], vec.tensor_scalar, T.tinb[:, 32:64], T.diagn[:], wcb[:, 1:2], None, ALU.mult)
-        t = V([t, t1], vec.transpose, T.toutb[:], T.tinb[:])
-        t_wr = V([t, t_rs], vec.tensor_tensor_scan, T.wrb[:], T.rs[:, 0:64], T.toutb[:], 0.0, ALU.mult, ALU.add)
-        t_wb = V([t_wr], vec.tensor_scalar, wb[:], T.wrb[:, 15:64:16], -0.015625, None, ALU.mult)
-
-        t_cs = [V([t_wb, t_dk[t], t_hs] + t_tk[b], vec.tensor_tensor, T.hs[:, t:256:4], T["dk%d" % t][:].indirect(wb[:]),
-                  T["tk%d" % t][:, NT * b:NT * b + NT], ALU.add) for t in range(4)]
-        t_n = V(t_cs, vec.quantize_mx, T[W[0]][:, 320:448], T[W[1]][:, 320:448], T.hs[:])
-        need("G", [t_n])
-        g.remote_dma(w8(W[0], 256, 320), w8(W[0], 320, 384), T.sem["rd%d" % b], T.sem.loc, pid, rid, mask)
-        g.remote_dma(T[W[1]][:, 256:320], T[W[1]][:, 320:384], T.sem["rd%d" % b], T.sem.loc, pid, rid, mask)
-
-        t_rb = A([t_wb, t_row], rb[:], T.row[:, 0:256].indirect(wb[:]))
-        ts = [A([t_wr], T.eqb[:, 64:260:65], T.wrb[:, 15:64:16], scale=-0.015625)]
-        ts += squares("eqb", 65, rb[:], "wrb", [t_wr, t_rb])
-        if b == 0:
-            t_hm = A([], T.hm[:], T.hz[:, 0:512])
-            cst["base"] = V([t_diag, t_row], vec.tensor_tensor, T.base[:], T.diag[:], T.row[:, 0:256], ALU.mult)
-            make_mk()
-            make_pj(0)
-            cst["step"] = V([t_row], vec.tensor_scalar, T.step[:], T.row[:, 0:80], 64.0, 1.0, ALU.is_lt, ALU.add)
-            t_tkm = [mx([t_x1, t_e1[i]] + t_sc, px(i, 0, 128), E1, 128 * i, XQ, 128, 128) for i in range(4)]
-            t_tk[1] = t_tk[2] = [A([t_tkm[t]], T["tk%d" % t][:, 64:192], px(t, 0, 128), scale=0.25) for t in range(4)]
-            make_ml(0)
-        arr_l = ("rl%d" % b, neng, {})
-        ta = [A([arr_l, t_dgn], T.tina[:, 32 * h:32 * h + 32], T.diagn[:], scale=wca[:, h:h + 1]) for h in range(2)]
-
-        t3 = V([t_row, t_diag], vec.tensor_tensor, T.t3[:], T.diag[:].indirect(wb[:]), T.row[:, 320:384], ALU.mult)
-        t = V(ta, vec.transpose, T.touta[:], T.tina[:])
-        t_d = V(ts + cst["mk"], vec.tensor_tensor_scan, T.dsb[:], T.mk[:], T.eqb[:], 100000.0, ALU.add, ALU.min)
-        t_wr = V([t], vec.tensor_tensor_scan, T.wra[:], T.rs[:, 0:64], T.touta[:], 0.0, ALU.mult, ALU.add)
-        tj = squares("eqj", 64, rb[:], "wra", [t_wr, t_rb])
-        t_ub = V([t_d], vec.tensor_scalar, ub[:], T.dsb[:, 64:260:65], 64.0, None, ALU.add)
-        t_wa = V([t_wr], vec.tensor_scalar, wa[:], T.wra[:, 15:64:16], -0.015625, None, ALU.mult)
-        t_ra = A([t_wa, t_row], T.ra[:], T.row[:, 0:256].indirect(wa[:]))
-        ts = [A([t_wr], T.eqa[:, 64:260:65], T.wra[:, 15:64:16], scale=-0.015625)]
-        ts += squares("eqa", 65, T.ra[:], "wra", [t_wr, t_ra])
-        t_vd = V([t_wa], vec.tensor_tensor, T.vd[:], T.diag[:].indirect(wa[:]), T.row[:, 256:320], ALU.mult)
-        t_ml = V([t3, t_ub, t_maps[b]], vec.tensor_copy, ml[:].indirect(ub[:]), T.t3[:])
-        t_j = V(tj + t_jm, vec.tensor_tensor_scan, T.dsj[:], T.jmk[:], T.eqj[:], 100000.0, ALU.add, ALU.min)
-        t_jl = V([t_j], vec.tensor_scalar, jl[:], T.dsj[:, 63:256:64], 63.0, 64.0, ALU.add, ALU.min)
-        t_p = pick(PJ, 64, 128, W, 320, 448, jl[:], [t_jl, t_pj[b]])
-        if b + 1 < R:
-            for h in range(2):
-                tr_scales(b + 1, h, t_x1)
-            make_ml(b + 1)
-        arr_d = ("rd%d" % b, 2 * neng, {})
-        for i in range(4):
-            mx([arr_d] + t_dk, pd(i, 0, 128), E1, 128 * i, W, 192, 128, True, False)
-        t_d = [mx(t_p, pd(i, 0, 128), E1, 128 * i, PJ, 0, 128, False, True) for i in range(4)]
-        t_cm = [A([t_d[i], t_hm], T.hm[:, i:512:8], pd(i, 64, 128), scale=0.5) for i in range(4)]
-        t = V(ts, vec.tensor_tensor_scan, T.dsa[:], T.mk[:], T.eqa[:], 100000.0, ALU.add, ALU.min)
-        t_va = V([t_jl, t_vd, cst["step"]], vec.tensor_tensor, T.va[:], T.step[:].indirect(jl[:]), T.vd[:], ALU.mult)
-        t_ua = V([t], vec.tensor_scalar, ua[:], T.dsa[:, 64:260:65], 64.0, None, ALU.add)
-        t = V([t_ua, t_va, t_ml], vec.tensor_copy, ml[:].indirect(ua[:]), T.va[:])
-        t = V([t], vec.tensor_tensor_scan, T.ls[:], T.rs[:], ml[:, 64:320], 0.0, ALU.mult, ALU.add)
-        if b == 0:
-            tr_codes(1, 0, t_x1)
-        t_ll = V([t], vec.tensor_copy, ll[:], T.ls[:, 15:256:16])
-        t_m = V(t_cm, vec.quantize_mx, T[W[0]][:, 512:640], T[W[1]][:, 512:640], T.hm[:])
-        dma("S", [t_rb], "st", T.ch[b:b + 1, 0:NT], rb[0:1, :])
-        if b + 1 < R:
-            t_tab = pick(("win%d" % (b + 1), "wins%d" % (b + 1)), 0, 256, W, 0, 640, ll[:], [t_m, t_ll])
-            make_pj(b + 1)
-            if b == 0:
-                tr_codes(1, 1, t_x1)
-
-    K = ("k3", "k3s")
-    t_h = [pick(K, 128 * m, 128 * m + 128, W, 0, 640, ll[:, 8 * m:8 * m + 8], [t_m, t_ll]) for m in range(2)]
-    t_y = [mx([t_wq] + t_h[m], T.ps[:, 512 * m:512 * m + 128], ("wq", "wqs"), 0, K, 128 * m, 128) for m in range(2)]
-    t_ya = A([t_y[0]], T.yt[:, 0:128], T.ps[:, 0:128])
-    dma("A", [t_ya], "st", T.y[:, 0:128], T.yt[:, 0:128])
-    t_yv = V([t_y[1]], vec.tensor_copy, T.yt[:, 128:256], T.ps[:, 512:640])
-    for m in range(2):
-        dma("S", t_h[m][0:1], "st", T.oc[:, 512 * m:512 * m + 512], w8("k3", 128 * m, 128 * m + 128))
-    for k in range(4):
-        dma("AASS"[k], t_h[1][1:2], "st", T.osc[4 * k:4 * k + 4, :], T.k3s[32 * k:32 * k + 4, :])
-    dma("S", [t_yv], "st", T.y[:, 128:256], T.yt[:, 128:256])
-    g.sync.wait_ge(T.sem.st, 16 * (R + 8))
-    g.wait_ge(T.sem.loc, 3 * R * neng)
+            total["c" + q] = count[q] = count.get(q, 0) + 1
+            o["fn"](*args, **kw).then_inc(T.sem["c" + q], 1)
+            token[name] = ("c" + q, count[q], dict(known[q]))
+    for sem, val in total.items():
+        if waited.get(sem, 0) < val:
+            (g if sem == "loc" else g.sync).wait_ge(T.sem[sem], val)

@@ -3,26 +3,21 @@ from concourse.mybir import dt, AluOpType, ActivationFunctionType
 ALU = AluOpType
 ACTF = ActivationFunctionType
 R = 3
-TKQ = "AAAA"
-DKQ = "VAAA"
-ODQ = "AAAA"
-CJQ = "AAAA"
-GQ = "V"
-YQ = "AVAV"
-OQ = "SSAASS"
-S = 512.0
-DROP = 321.0 * S
-HUGE = 1.0e6
+CFG = {"tc": "AAAA", "dc": "VAAA" * 3, "od": "VVAA" * 3, "cj": "AAAA" * 3, "co": "AAAA" * 3, "ca": "aavv" * 3, "la": "AVV", "ea": "A",
+       "y": "AVAV", "o": "SASSAA", "oc": "SS", "lk": "AS", "k": "AAA", "raw": "100"}
+S = 32.0
+BIG = S * S
+HUGE = 4096.0
+TB = 320
 ALL = (0, 128)
 
 X4 = "float8_e4m3fn_x4"
 SCRATCH = {"pa": ("psum", [128, 2048], "float32"), "pb": ("psum", [128, 2048], "float32"),
-           "pidx": ("sbuf", [128, 1], "int32"), "pand": ("sbuf", [128, 1], "int32"), "rep": ("sbuf", [128, 8], "uint16")}
-for _n, _w in (("xt", 512), ("xr", 1024), ("kt", 1024), ("wt", 512), ("z", 516), ("h", 768), ("sg", 256)):
+           "pidx": ("sbuf", [128, 1], "int32"), "pand": ("sbuf", [128, 2], "int32"), "rep": ("sbuf", [128, 16], "uint16")}
+for _n, _w in (("xt", 512), ("kt", 1024), ("wt", 512), ("z", 516), ("h", 768), ("sg", 256), ("m5", 260), ("m6", 264), ("eo", 260),
+               ("so", 260), ("ej", 260), ("sj", 260), ("sk", 68), ("ea", 264), ("sa", 264)):
     SCRATCH[_n] = ("sbuf", [128, _w], "bfloat16")
-for _n, _w in (("qc", 1), ("qm", 1), ("adj", 1), ("c16", 256), ("row", 448), ("iq", 260), ("mk", 260), ("fm", 256), ("vf", 64),
-               ("pm", 256), ("wc", 1), ("repi", 8), ("eqb", 260), ("dsb", 260), ("eqa", 260), ("dsa", 260), ("ra", 64),
-               ("gr", 64), ("gs", 64), ("va", 64), ("ls", 256), ("yw", 512), ("yt", 256)):
+for _n, _w in (("qc", 2), ("row", 256), ("pm", 256), ("repi", 16), ("uc", 4), ("us", 4), ("af", 4), ("rb", 192), ("yw", 512), ("yt", 256)):
     SCRATCH[_n] = ("sbuf", [128, _w], "float32")
 for _t in range(4):
     for _n, _w in (("dk", 256), ("tk", 192), ("od", 65), ("cj", 64)):
@@ -31,26 +26,26 @@ for _n, _w in (("e", 512), ("xq", 256), ("tr", 384), ("wq", 128), ("win0", 576),
     SCRATCH[_n] = ("sbuf", [128, _w], X4)
     SCRATCH[_n + "s"] = ("sbuf", [128, _w], "uint8")
 for _b in range(R):
-    for _n, _w in (("wb", 4), ("wa", 4), ("ub", 4), ("ua", 4), ("jl", 4), ("ll", 16)):
+    for _n, _w in (("wb", 4), ("wa", 4), ("jl", 4), ("ll", 16)):
         SCRATCH["%s%d" % (_n, _b)] = ("sbuf", [128, _w], "uint16")
-    for _n, _w in (("ml", 320), ("rb", 64)):
-        SCRATCH["%s%d" % (_n, _b)] = ("sbuf", [128, _w], "float32")
+    for _n in ("wc", "wr"):
+        SCRATCH["%s%d" % (_n, _b)] = ("sbuf", [128, 4], "float32")
 
-SEMAPHORES = ["cV", "cA", "cP", "cG", "lx0", "lx1", "lr1", "lr2", "lk", "lw", "st", "loc"]
+SEMAPHORES = ["cV", "cA", "cP", "cG", "lx0", "lx1", "lk0", "lk1", "lw", "st", "loc"]
 for _b in range(R):
-    SEMAPHORES += ["rl%d" % _b, "rd%d" % _b, "lm%d" % _b]
+    SEMAPHORES += ["rl%d" % _b, "rd%d" % _b]
 
-ORDER = """repi lx01 pidx z0 lk lx10 z1 lr10 lr11 c16 lr12 iq lr13 h0 pand qc qx0 lr14 row lr20 lr21 rep e3 tk03 e2 t0s eqb0 t0c lr22 lr23 qk adj
-e1 lr24 ml1 tk02 qx1 e0 eqa0 qm sc0 tc02 tk01 pm0 mk0 fm0 tc03 tc01 tk00 sg0 la01 la02 la00 la03 du01 du02 mk2 tc00 ml0 lb03 lb02 lb01 du03
-du00 sl0 mk1 dc01 dc02 dc00 dc03 sh02 wf0 rb0 b0q2 b0q1 sh01 b0q0 al0 sh00 sh03 sq0 b0q3 qr2 b0s ou00 fm1 ou03 ou02 sc_0 ou01 od00 od02 od01
-b0u ra0 qr1 mb0 af0 ss_0 gr0 od03 a0q3 a0q1 a0q2 a0q0 ad0 tk13 tk10 vf0 gs0 jl0 a0s au02 au00 va0 lw a0u cj00 cj02 ma0 mh02 cj03 cj01 tc10
-au03 mh00 mh03 au01 mh01 ls0 ml2 tk12 tk11 tc12 tc13 tc11 mq0 ll0 tp0s tp0c sc1 pm1 du10 dc10 du12 du11 du13 qw sg1 la11 la10 la12 la13 lb12
-lb13 lb11 dc11 dc12 dc13 wf1 sh12 sl1 rb1 b1q0 b1q2 b1q1 sh10 sh13 sh11 sq1 b1q3 sc_1 ss_1 b1s ad1 al1 ra1 b1u af1 mb1 ou12 gr1 vf1 ou10 ou13
-ou11 a1q2 a1q3 a1q1 a1q0 od11 od10 a1s gs1 od12 od13 au10 va1 jl1 a1u cj10 cj13 cj11 cj12 au13 au11 au12 ma1 ch0 mh10 ls1 mh11 mh13 mh12 ll1
-mq1 tp1s tp1c sc2 du20 du23 pm2 sg2 dc20 du21 dc23 la23 du22 dc22 dc21 la20 la22 la21 lb22 lb21 lb23 sl2 wf2 sh20 sh23 sh21 sh22 sq2 ou23 ou22
-sc_2 ou21 ou20 ss_2 rb2 b2q1 b2q2 b2q3 al2 ad2 au23 au22 b2q0 b2s b2u ra2 af2 od23 ch1 a2q1 a2q0 a2q2 od21 a2q3 mb2 od20 au21 au20 ch2 y0 gr2
-vf2 gs2 a2s jl2 od22 va2 cj22 cj23 cj20 y1 a2u ma2 cj21 mh23 mh22 ls2 mh20 mh21 yc0 ll2 mq2 tp2s yc1 y2 tp2c oc os2 yc2 yp1 yp0 os0 oy0 oy1
-os3 os1"""
+ORDER = """pidx lx0 z03 lk0 z00 lk1 repi z02 lx1 h0 lw z1 pblk pand z01 qc row rep e0 m6a qx0 eac e1 ejc m6c t0c tk00 m6b t0s tk01 qk0 tc00 e2 m5a
+qk1 sc00 e3 tk02 tc01 sc01 pm00 m5c m5b uc tk03 tc02 du00 pm01 eoc qx1 tc03 du02 sg0 dc00 du01 us du03 sl0 l0a1 l0a3 al0 l0a2 dc02 l0b1 l0b0
+dc01 l0b3 l0b2 dc03 sh00 sh02 rb0 sh01 sh03 co00 co02 sq0 co03 t1c co01 t1s sc_0 ou00 ou03 so0 ou01 od00 ou02 od03 ss_0 ad0 tk10 tk13 w0a1 cq0
+ea0 w0a3 od02 w0a2 od01 sj0 w0b0 tk12 w0b1 w0b2 j0a1 w0b3 tk11 j0a3 j0a2 fa0 ca03 ca01 j0b3 ca00 au00 j0b1 j0b0 j0b2 au01 tc11 ca02 au02 cj01
+au03 sa0 cj00 cj02 mh01 lc03 cj03 lc02 lc00 lc01 tc10 mh02 mh00 tc12 mh03 ld02 ld01 tc13 ld03 mq0 tp00c tp00s tp01c tp01s sc10 sc11 pm10 du10
+pm11 du11 dc10 du13 sg1 du12 l1a1 l1a2 l1a3 dc11 l1b2 l1b0 dc12 l1b3 l1b1 dc13 sh11 sl1 al1 sh10 rb1 sh12 sh13 co12 co10 sq1 co11 co13 sc_1
+ou12 ou13 ou11 ou10 af1 ca10 ca12 od12 ss_1 ad1 cq10 od13 cq13 cq11 ca11 cq12 so1 ca13 sj1 ea1 fa1 od11 jl1 sa1 od10 cj13 lc10 cj12 lc12 lc13
+lc11 cj10 qw au10 cj11 ld13 au12 ld11 ld12 au13 mh10 au11 mh12 mh13 mh11 mq1 tp10c tp10s tp11c tp11s sc20 sc21 pm20 du20 pm21 du22 dc20 du21
+sg2 du23 l2a1 l2a2 l2a3 dc22 l2b1 l2b3 dc23 l2b0 l2b2 dc21 sh22 sl2 al2 sh20 rb2 sh23 sh21 ch co20 co21 sq2 co22 co23 sc_2 ou22 ou23 ou20 ou21
+af2 ca20 ca22 od22 ss_2 ad2 cq22 ca21 cq20 cq23 od23 cq21 so2 ca23 sj2 ea2 fa2 od21 jl2 sa2 od20 cj23 lc21 cj22 lc22 lc20 lc23 cj20 au22 cj21
+ld21 au23 ld22 au21 mh22 ld23 au20 mh23 y0 mh21 mh20 y1 mq2 yc0 yc1 tp20c y2 tp20s tp21c yc2 oc0 tp21s yp1 oc1 yp0 os0 os1 oy1 oy0 os3 os2"""
 
 
 def X(name, a=0, b=None, step=1, part=ALL, cast=None, off=None):
@@ -89,8 +84,8 @@ def plan(g, T):
     def A(name, out, in_, func=ACTF.Copy, **kw):
         op(name, "A", act.activation, (out, in_, func), kw, [out] + ([kw["accum_out"]] if "accum_out" in kw else []))
 
-    def iota(name, out, pattern):
-        G(name, g.iota, out, pattern, 0, 0, allow_small_or_imprecise_dtypes=True)
+    def iota(name, out, pattern, base=0):
+        G(name, g.iota, out, pattern, base, 0, allow_small_or_imprecise_dtypes=True)
 
     def quant(name, buf, a, b, tile):
         c, s = X(buf, a, b), X(buf + "s", a, b)
@@ -99,9 +94,9 @@ def plan(g, T):
     def mx(name, out, st, a, mv, c, n):
         op(name, "P", ten.matmul_mx, (out, X(st, a, a + 128), X(st + "s", a, a + 128), X(mv, c, c + n), X(mv + "s", c, c + n), True, True), {}, [out])
 
-    def pick(name, out, a, b, win, n, off):
-        V(name + "c", vec.tensor_copy, X(out, a, b, cast=dt.uint32), X(win, 0, n, cast=dt.uint32, off=off))
-        A(name + "s", X(out + "s", a, b), X(win + "s", 0, n, off=off))
+    def pick(name, out, a, b, win, c, d, off):
+        V(name + "c", vec.tensor_copy, X(out, a, b, cast=dt.uint32), X(win, c, d, cast=dt.uint32, off=off))
+        A(name + "s", X(out + "s", a, b), X(win + "s", c, d, off=off))
 
     def dma(name, q, sem, out, in_):
         op(name, q, (g.sync if q == "S" else act).dma_start, (out, in_), {}, [out] if is_view(out) else [], sem, "d")
@@ -120,125 +115,152 @@ def plan(g, T):
         else:
             V(name, vec.tensor_scalar, out, in_, f, None, ALU.mult)
 
-    def fold(name, out, in_, n):
-        V(name, vec.tensor_tensor_scan, out, X("fm", 0, n), in_, 0.0, ALU.add, ALU.min)
+    def differ(name, q, out, row, plain, scaled):
+        if q in "Aa":
+            A(name, out, row, ACTF.Square, bias=scaled, scale=-S)
+        else:
+            V(name, vec.tensor_scalar, out, row, plain, BIG, ALU.not_equal, ALU.mult)
 
-    def places(name, eq, ds, row, out):
+    def fill(name, q, out, n, value):
+        if q == "G":
+            iota(name, out, [[0, n]], int(value))
+        elif q == "V":
+            V(name, vec.memset, out, float(value))
+        else:
+            A(name, out, X("z", 0, n), scale=0.0, bias=float(value))
+
+    def spread(name, out, buf, c, add=None):
+        for k in range(1, 4):
+            copy("%sa%d" % (name, k), CFG["la"][k - 1], X(buf, c + k, c + k + 1, part=block(0)), X(buf, c, c + 1, part=block(k)))
         for k in range(4):
-            n = 16 * k + 16
-            A("%sq%d" % (name, k), X(eq, 65 * k, 65 * k + n), X(row, 0, n), ACTF.Square, bias=X(eq, 65 * k + 64, 65 * k + 65), scale=-S)
-        V(name + "s", vec.tensor_tensor_scan, X(ds), X("mk"), X(eq), HUGE, ALU.add, ALU.min)
-        V(name + "u", vec.tensor_scalar, X(out), X(ds, 64, 260, 65), 1.0 / S, 64.0, ALU.mult, ALU.add)
+            if add is None:
+                V("%sb%d" % (name, k), vec.tensor_copy, X(out, part=block(k)), X(buf, c, c + 4, part=block(0)))
+            else:
+                V("%sb%d" % (name, k), vec.tensor_scalar, X(out, part=block(k)), X(buf, c, c + 4, part=block(0)), add, None, ALU.add)
 
     def bank(buf, t, a, b):
         return X(buf, 512 * t + a, 512 * t + b)
 
-    dma("lx01", "S", "lx0", X("h", 0, 256), T.x[:, 0:256])
-    dma("lk", "A", "lk", X("kt"), T.kb[:])
-    dma("lx10", "S", "lx1", X("xt"), T.x[:, 256:768])
-    for b in (1, 2):
-        for i in range(5):
-            a, c = max(128 * i - 64, 0), min(128 * i + 64, 512)
-            s = 256 * b + max(64 * i - 64, 0)
-            dma("lr%d%d" % (b, i), "S", "lr%d" % b, X("xr", 512 * b - 512 + a, 512 * b - 512 + c), T.x[:, s:s + c - a])
+    def block(k):
+        return (32 * k, 32 * k + 32)
+
+    dma("lx0", "S", "lx0", X("h", 0, 256), T.x[:, 0:256])
+    for m in range(2):
+        dma("lk%d" % m, CFG["lk"][m], "lk%d" % m, X("kt", 512 * m, 512 * m + 512), T.kb[:, 512 * m:512 * m + 512])
+    dma("lx1", "S", "lx1", X("xt"), T.x[:, 256:768])
     dma("lw", "S", "lw", X("wt"), T.w[:])
 
-    V("z0", vec.memset, X("z"), 0.0)
-    G("pidx", g.iota, X("pidx"), [[0, 1]], 0, 1)
+    for t in range(4):
+        V("z0%d" % t, vec.memset, X("z", t, 516, 4), 0.0)
+    G("pidx", g.iota, X("pidx"), [[0, 1]], 0, 2)
     G("z1", g.affine_select, X("z", 3, 515, 4), X("z", 3, 515, 4), [[-1, 128]], ALU.not_equal, 0.5, 0, 1)
     V("h0", vec.memset, X("h", 256, 512), 0.0)
     for t in range(4):
         quant("e%d" % t, "e", 128 * t, 128 * t + 128, X("z", 3 - t, 515 - t))
-    iota("c16", X("c16"), [[0, 16], [1, 16]])
     quant("qx0", "xq", 0, 128, X("h", 0, 512))
-    quant("qk", "win0", 0, 256, X("kt"))
-    V("pand", vec.tensor_scalar, X("pand"), X("pidx"), 15, None, ALU.bitwise_and)
+    for m in range(2):
+        quant("qk%d" % m, "win0", TB + 128 * m, TB + 128 * m + 128, X("kt", 512 * m, 512 * m + 512))
+    V("pand", vec.tensor_scalar, X("pand", 0, 1), X("pidx"), 1, 15, ALU.logical_shift_right, ALU.bitwise_and)
+    V("pblk", vec.tensor_scalar, X("pand", 1, 2), X("pidx"), 192, None, ALU.bitwise_and)
     V("qc", vec.tensor_copy, X("qc"), X("pand"))
-    iota("repi", X("repi"), [[16, 4], [0, 2]])
-    V("rep", vec.tensor_scalar, X("rep"), X("repi"), X("qc"), None, ALU.add)
-    pick("t0", "tr", 0, 128, "xq", 128, X("rep"))
-    V("adj", vec.tensor_scalar, X("adj"), X("qc"), -1000.0, 15000.0, ALU.mult, ALU.add)
-    V("fm0", vec.tensor_scalar, X("fm"), X("c16"), X("qc"), 101000.0, ALU.is_equal, ALU.mult)
-    A("fm1", X("fm"), X("fm"), bias=-1000.0)
-    iota("iq", X("iq"), [[-16, 4], [1, 65]])
-    iota("row", X("row"), [[1, 448]])
-    V("mk0", vec.tensor_scalar, X("mk"), X("iq"), X("qc"), -DROP, ALU.is_equal, ALU.mult)
-    V("qm", vec.tensor_scalar, X("qm"), X("qc"), S, DROP, ALU.mult, ALU.add)
-    V("mk1", vec.tensor_scalar, X("mk", 65, 260, 65), X("iq", 65, 260, 65), 0.0, HUGE, ALU.mult, ALU.add)
-    V("mk2", vec.tensor_scalar, X("mk", 64, 260, 65), X("iq", 64, 260, 65), -S, X("qm"), ALU.mult, ALU.add)
-    A("eqb0", X("eqb", 0, 195), X("h", 256, 451))
-    A("eqa0", X("eqa", 0, 195), X("h", 256, 451))
-    for b in range(R):
-        dma("ml%d" % b, "S", "lm%d" % b, X("ml%d" % b, 64, 320), X("row", 0, 256))
+    iota("repi", X("repi"), [[16, 8], [0, 2]])
+    V("rep", vec.tensor_scalar, X("rep"), X("repi"), X("qc", 0, 1), None, ALU.add)
+    pick("t0", "tr", 0, 128, "xq", 0, 128, X("rep", 0, 8))
+    iota("row", X("row"), [[1, 256]])
+    V("uc", vec.tensor_scalar, X("uc"), X("repi", 0, 8, 2), X("qc", 0, 1), X("qc", 1, 2), ALU.add, ALU.add)
+    A("us", X("us"), X("uc"), scale=S)
+    A("eoc", X("eo", 64, 260, 65), X("uc"))
+    for name, w, end in (("m5", 65, -65), ("m6", 66, -129)):
+        fill(name + "a", CFG["k"][0], X(name), 4 * w, -1)
+        fill(name + "b", CFG["k"][1], X(name, 0, 4 * w, w), 4, HUGE)
+        fill(name + "c", CFG["k"][1], X(name, 64, 4 * w, w), 4, end)
+    fill("ejc", CFG["k"][2], X("ej", 64, 260, 65), 4, -64)
+    fill("eac", CFG["k"][2], X("ea", 64, 264, 66), 4, HUGE)
     quant("qx1", "xq", 128, 256, X("xt"))
-    quant("qr1", "tr", 128, 256, X("xr", 0, 512))
-    quant("qr2", "tr", 256, 384, X("xr", 512, 1024))
+    pick("t1", "tr", 128, 384, "xq", 128, 256, X("rep"))
     quant("qw", "wq", 0, 128, X("wt"))
 
     for b in range(R):
         W, N, n = "win%d" % b, "win%d" % (b + 1), str(b)
-        wb, wa, ub, ua, jl, ll, ml, rb = [nm + n for nm in ("wb", "wa", "ub", "ua", "jl", "ll", "ml", "rb")]
+        wb, wa, jl, ll, wc, wr = [nm + n for nm in ("wb", "wa", "jl", "ll", "wc", "wr")]
+        raw = CFG["raw"][b] == "1"
+        rb = X("rb", 64 * b, 64 * b + 64)
 
-        mx("sc" + n, bank("pb", 0, 0, 256), "tr", 128 * b, W, 0, 256)
-        V("pm" + n, vec.tensor_tensor_scan, X("pm"), X("h", 256, 512), bank("pb", 0, 0, 256), -1.0e29, ALU.add, ALU.max)
+        for m in range(2):
+            mx("sc%d%d" % (b, m), bank("pb", m, 0, 128), "tr", 128 * b, W, TB + 128 * m, 128)
+            V("pm%d%d" % (b, m), vec.tensor_tensor_scan, X("pm", 128 * m, 128 * m + 128), X("h", 256, 384), bank("pb", m, 0, 128),
+              X("pm", 127, 128) if m else -1.0e29, ALU.add, ALU.max)
         for t in range(4):
             if b < 2:
                 mx("tk%d%d" % (b, t), bank("pa", t, 0, 128), "e", 128 * t, "xq", 128 * b, 128)
-                copy("tc%d%d" % (b, t), TKQ[t], X("tk%d" % t, 64 * b, 128 * b + 64), bank("pa", t, 0, 64 * b + 64), 0.5)
-            mx("du%d%d" % (b, t), bank("pa", t, 0, 256), "e", 128 * t, W, 0, 256)
-            copy("dc%d%d" % (b, t), DKQ[t], X("dk%d" % t), bank("pa", t, 0, 256), 1.5)
-        A("sg" + n, X("sg"), X("pm"), ACTF.Sign, bias=X("pm", 255, 256), scale=-1.0, accum_out=X("wc"))
+                copy("tc%d%d" % (b, t), CFG["tc"][t], X("tk%d" % t, 64 * b, 128 * b + 64), bank("pa", t, 0, 64 * b + 64), 0.5)
+            mx("du%d%d" % (b, t), bank("pa", t, 0, 256), "e", 128 * t, W, TB, 256)
+            copy("dc%d%d" % (b, t), CFG["dc"][4 * b + t], X("dk%d" % t), bank("pa", t, 0, 256), 1.5)
+        A("sg" + n, X("sg"), X("pm"), ACTF.Sign, bias=X("pm", 255, 256), scale=-1.0, accum_out=X(wc, 0, 1))
+        spread("l" + n, wb, wc, 0)
+        if raw:
+            send("sl" + n, "rl" + n, X(wr, 0, 1), X(wc, 0, 1))
+        else:
+            send("sl" + n, "rl" + n, X(wa), X(wb))
+
+        for t in range(4):
+            V("sh%d%d" % (b, t), vec.tensor_tensor, X("h", t, 256, 4), X("dk%d" % t, off=X(wb)), X("tk%d" % t, 64 * b, 64 * b + 64), ALU.add)
+        quant("sq" + n, W, 192, 320, X("h", 0, 512))
+        send("sc_" + n, "rd" + n, X(W, 128, 192, cast=dt.uint8), X(W, 192, 256, cast=dt.uint8))
+        send("ss_" + n, "rd" + n, X(W + "s", 128, 192), X(W + "s", 192, 256))
+
+        A("rb" + n, rb, X("row", off=X(wb)))
         for k in range(4):
-            V("la%d%d" % (b, k), vec.tensor_copy, X(wb, k, k + 1, part=(0, 32)), X("wc", part=(32 * k, 32 * k + 32)))
+            differ("co%d%d" % (b, k), CFG["co"][4 * b + k], X("eo", 65 * k, 65 * k + 64), rb, X("uc", k, k + 1), X("us", k, k + 1))
+        V("so" + n, vec.tensor_tensor_scan, X("so"), X("m5"), X("eo"), 0.0, ALU.add, ALU.min)
+        copy("ea" + n, CFG["ea"], X("ea", 65, 264, 66), X("so", 64, 260, 65))
+        V("fa" + n, vec.tensor_scalar, X("m6", 65, 264, 66), X("so", 64, 260, 65), 0.0, -64.0, ALU.is_lt, ALU.mult)
+
+        if raw:
+            landed("al" + n, "rl" + n, [X(wr)], ["sl" + n])
+            differ("cq" + n, "V", X("ej", 0, 64), rb, X(wr, 0, 1), None)
+            V("sj" + n, vec.tensor_tensor_scan, X("sk", 0, 65), X("m5", 0, 65), X("ej", 0, 65), 0.0, ALU.add, ALU.min)
+            spread("j" + n, jl, "sk", 64, 128.0)
+            spread("w" + n, wa, wr, 0)
+        else:
+            landed("al" + n, "rl" + n, [X(wa)], ["sl" + n])
+            V("af" + n, vec.tensor_copy, X("af"), X(wa))
+            for k in range(4):
+                differ("cq%d%d" % (b, k), "V", X("ej", 65 * k, 65 * k + 64), rb, X("af", k, k + 1), None)
+            V("sj" + n, vec.tensor_tensor_scan, X("sj"), X("m5"), X("ej"), 0.0, ALU.add, ALU.min)
+            V("jl" + n, vec.tensor_scalar, X(jl), X("sj", 64, 260, 65), 128.0, None, ALU.add)
+        for t in range(4):
+            mx("ou%d%d" % (b, t), bank("pa", t, 0, 128), "e", 128 * t, W, 192, 128)
+            copy("od%d%d" % (b, t), CFG["od"][4 * b + t], X("od%d" % t), bank("pa", t, 0, 65))
+            copy("cj%d%d" % (b, t), CFG["cj"][4 * b + t], X("cj%d" % t), X("od%d" % t, off=X(jl)))
+
+        for k in range(4):
+            differ("ca%d%d" % (b, k), CFG["ca"][4 * b + k], X("ea", 66 * k, 66 * k + 64), X("row", off=X(wa)), X("uc", k, k + 1), X("us", k, k + 1))
+        V("sa" + n, vec.tensor_tensor_scan, X("sa"), X("m6"), X("ea"), 0.0, ALU.add, ALU.min)
+        for k in range(4):
+            V("lc%d%d" % (b, k), vec.tensor_scalar, X(ll, 4 * k, 4 * k + 4, part=block(0)), X("sa", 65, 264, 66, part=block(k)), 256.0, None, ALU.add)
         for k in range(1, 4):
-            V("lb%d%d" % (b, k), vec.tensor_copy, X(wb, part=(32 * k, 32 * k + 32)), X(wb, part=(0, 32)))
-        send("sl" + n, "rl" + n, X(wa), X(wb))
+            V("ld%d%d" % (b, k), vec.tensor_copy, X(ll, part=block(k)), X(ll, part=block(0)))
 
+        landed("ad" + n, "rd" + n, [X(W, 128, 192), X(W + "s", 128, 192)], ["sc_" + n, "ss_" + n])
         for t in range(4):
-            V("sh%d%d" % (b, t), vec.tensor_tensor, X("h", 512 + t, 768, 4), X("dk%d" % t, off=X(wb)), X("tk%d" % t, 64 * b, 64 * b + 64), ALU.add)
-        quant("sq" + n, W, 256, 384, X("h", 256, 768))
-        send("sc_" + n, "rd" + n, X(W, 384, 448, cast=dt.uint8), X(W, 320, 384, cast=dt.uint8))
-        send("ss_" + n, "rd" + n, X(W + "s", 384, 448), X(W + "s", 320, 384))
+            mx("au%d%d" % (b, t), bank("pb", t, 0, 128), "e", 128 * t, W, 128, 128)
+            V("mh%d%d" % (b, t), vec.tensor_tensor, X("h", 512 + t, 768, 4), bank("pb", t, 0, 64), X("cj%d" % t), ALU.add)
+        quant("mq" + n, W, 0, 128, X("h", 256, 768))
+        c = TB if b < R - 1 else 0
+        for m in range(2):
+            pick("tp%d%d" % (b, m), N, c + 128 * m, c + 128 * m + 128, W, 64, 576, X(ll, 8 * m, 8 * m + 8))
 
-        A("rb" + n, X(rb), X("row", 0, 256, off=X(wb)))
-        V("wf" + n, vec.tensor_scalar, X("eqb", 64, 260, 65), X(wb), S, None, ALU.mult)
-        places("b" + n, "eqb", "dsb", rb, ub)
-        V("mb" + n, vec.tensor_copy, X(ml, off=X(ub)), X("row", 320, 384))
-        dma("ch" + n, "S", "st", T.ch[b:b + 1, 0:64], X(rb, part=(0, 1)))
-
-        landed("al" + n, "rl" + n, [X(wa)], ["sl" + n])
-        copy("gr" + n, GQ, X("gr"), X(ml, 64, 320, off=X(wa)))
-        fold("gs" + n, X("gs"), X("gr"), 64)
-        V("jl" + n, vec.tensor_scalar, X(jl), X("gs", 15, 64, 16), X("adj"), -319.0, ALU.add, ALU.add)
-        for t in range(4):
-            mx("ou%d%d" % (b, t), bank("pa", t, 0, 128), "e", 128 * t, W, 256, 128)
-            copy("od%d%d" % (b, t), ODQ[t], X("od%d" % t), bank("pa", t, 63, 128))
-            copy("cj%d%d" % (b, t), CJQ[t], X("cj%d" % t), X("od%d" % t, off=X(jl)))
-        V("vf" + n, vec.tensor_scalar, X("vf"), X(ml, 64, 320, off=X(wa)), 320.0, 64.0, ALU.is_ge, ALU.mult)
-        V("va" + n, vec.tensor_tensor, X("va"), X("vf"), X("row", 384, 448), ALU.add)
-        A("ra" + n, X("ra"), X("row", 0, 256, off=X(wa)))
-        V("af" + n, vec.tensor_scalar, X("eqa", 64, 260, 65), X(wa), S, None, ALU.mult)
-        places("a" + n, "eqa", "dsa", "ra", ua)
-        V("ma" + n, vec.tensor_copy, X(ml, off=X(ua)), X("va"))
-        fold("ls" + n, X("ls"), X(ml, 64, 320), 256)
-        V("ll" + n, vec.tensor_scalar, X(ll), X("ls", 15, 256, 16), X("adj"), None, ALU.add)
-
-        landed("ad" + n, "rd" + n, [X(W, 384, 448), X(W + "s", 384, 448)], ["sc_" + n, "ss_" + n])
-        for t in range(4):
-            mx("au%d%d" % (b, t), bank("pb", t, 0, 128), "e", 128 * t, W, 320, 128)
-            V("mh%d%d" % (b, t), vec.tensor_tensor, X("h", t, 256, 4), bank("pb", t, 64, 128), X("cj%d" % t), ALU.add)
-        quant("mq" + n, W, 448, 576, X("h", 0, 512))
-        pick("tp" + n, N, 0, 256, W, 512, X(ll))
-
-    for i, (a, c) in enumerate(((0, 320), (320, 448), (448, 576))):
+    dma("ch", "S", "st", T.ch[:], X("rb", part=(0, 1)))
+    for i, (a, c, u) in enumerate(((TB, 576, 0), (128, 256, 0), (0, 128, 64))):
         mx("y%d" % i, bank("pa", i, 0, c - a), "wq", 0, W, a, c - a)
-        copy("yc%d" % i, YQ[i], X("yw", a, min(c, 512)), bank("pa", i, 0, min(c, 512) - a))
+        copy("yc%d" % i, CFG["y"][i], X("yw", a + u - 64, c - 64), bank("pa", i, u, c - a))
     for m in range(2):
-        copy("yp%d" % m, YQ[2 + m], X("yt", 128 * m, 128 * m + 128), X("yw", off=X(ll, 8 * m, 8 * m + 8)))
-        dma("oy%d" % m, OQ[m], "st", T.y[:, 128 * m:128 * m + 128], X("yt", 128 * m, 128 * m + 128))
-    dma("oc", "S", "st", T.oc[:], X(N, cast=dt.uint8))
+        copy("yp%d" % m, CFG["y"][2 + m], X("yt", 128 * m, 128 * m + 128), X("yw", off=X(ll, 8 * m, 8 * m + 8)))
+        dma("oy%d" % m, CFG["o"][m], "st", T.y[:, 128 * m:128 * m + 128], X("yt", 128 * m, 128 * m + 128))
+        dma("oc%d" % m, CFG["oc"][m], "st", T.oc[:, 512 * m:512 * m + 512], X(N, 128 * m, 128 * m + 128, cast=dt.uint8))
     for k in range(4):
-        dma("os%d" % k, OQ[2 + k], "st", T.osc[4 * k:4 * k + 4, :], X(N + "s", part=(32 * k, 32 * k + 4)))
+        dma("os%d" % k, CFG["o"][2 + k], "st", T.osc[4 * k:4 * k + 4, :], X(N + "s", part=(32 * k, 32 * k + 4)))
 
     for i, o in enumerate(ops):
         o["deps"] = []

@@ -3,8 +3,11 @@ from concourse.mybir import dt, AluOpType, ActivationFunctionType
 ALU = AluOpType
 ACTF = ActivationFunctionType
 R = 3
-CFG = {"tc": "AAAA", "dc": "VAAA" * 3, "od": "VVAA" * 3, "cj": "AAAA" * 3, "co": "AAAA" * 3, "ca": "aavv" * 3, "la": "AVV", "ea": "A",
-       "y": "AVAV", "o": "SASSAA", "oc": "SS", "lk": "AS", "k": "AAA", "raw": "100"}
+CUT = (256, 64, 64, 128)
+HALVED = (1, 2)
+BT = 3
+SUMMED = ((), (3,), (3,))
+STORES = "SSAA"
 S = 32.0
 BIG = S * S
 HUGE = 4096.0
@@ -13,16 +16,16 @@ ALL = (0, 128)
 
 X4 = "float8_e4m3fn_x4"
 SCRATCH = {"pa": ("psum", [128, 2048], "float32"), "pb": ("psum", [128, 2048], "float32"),
-           "pidx": ("sbuf", [128, 1], "int32"), "pand": ("sbuf", [128, 2], "int32"), "rep": ("sbuf", [128, 16], "uint16")}
-for _n, _w in (("xt", 512), ("kt", 1024), ("wt", 512), ("z", 516), ("h", 768), ("sg", 256), ("m5", 260), ("m6", 264), ("eo", 260),
-               ("so", 260), ("ej", 260), ("sj", 260), ("sk", 68), ("ea", 264), ("sa", 264)):
+           "pidx": ("sbuf", [128, 1], "int32"), "pand": ("sbuf", [128, 2], "int32"), "rep": ("sbuf", [128, 8], "uint16")}
+for _n, _w in (("xt", 512), ("kt", 1024), ("wt", 512), ("z", 516), ("z2", 516), ("h", 768), ("sg", 256), ("m5", 260), ("m6", 264), ("eo", 260),
+               ("so", 260), ("ej", 260), ("sk", 68), ("ea", 264), ("sa", 264)):
     SCRATCH[_n] = ("sbuf", [128, _w], "bfloat16")
-for _n, _w in (("qc", 2), ("row", 256), ("pm", 256), ("repi", 16), ("uc", 4), ("us", 4), ("af", 4), ("rb", 192), ("yw", 512), ("yt", 256)):
+for _n, _w in (("qc", 2), ("row", 256), ("pm", 256), ("repi", 8), ("uc", 4), ("us", 4), ("rb", 192), ("yw", 512), ("yt", 256), ("sx", 64)):
     SCRATCH[_n] = ("sbuf", [128, _w], "float32")
 for _t in range(4):
     for _n, _w in (("dk", 256), ("tk", 192), ("od", 65), ("cj", 64)):
         SCRATCH["%s%d" % (_n, _t)] = ("sbuf", [128, _w], "float32")
-for _n, _w in (("e", 512), ("xq", 256), ("tr", 384), ("wq", 128), ("win0", 576), ("win1", 576), ("win2", 576), ("win3", 256)):
+for _n, _w in (("e", 640), ("xq", 256), ("tr", 384), ("wq", 128), ("win0", 576), ("win1", 576), ("win2", 576), ("win3", 256)):
     SCRATCH[_n] = ("sbuf", [128, _w], X4)
     SCRATCH[_n + "s"] = ("sbuf", [128, _w], "uint8")
 for _b in range(R):
@@ -33,19 +36,24 @@ for _b in range(R):
 
 SEMAPHORES = ["cV", "cA", "cP", "cG", "lx0", "lx1", "lk0", "lk1", "lw", "st", "loc"]
 for _b in range(R):
-    SEMAPHORES += ["rl%d" % _b, "rd%d" % _b]
+    SEMAPHORES += ["rl%d" % _b, "rd%d" % _b, "rx%d" % _b]
 
-ORDER = """pidx lx0 z03 lk0 z00 lk1 repi z02 lx1 h0 lw z1 pblk pand z01 qc row rep e0 m6a qx0 eac e1 ejc m6c t0c tk00 m6b t0s tk01 qk0 tc00 e2 m5a
-qk1 sc00 e3 tk02 tc01 sc01 pm00 m5c m5b uc tk03 tc02 du00 pm01 eoc qx1 tc03 du02 sg0 dc00 du01 us du03 sl0 l0a1 l0a3 al0 l0a2 dc02 l0b1 l0b0
-dc01 l0b3 l0b2 dc03 sh00 sh02 rb0 sh01 sh03 co00 co02 sq0 co03 t1c co01 t1s sc_0 ou00 ou03 so0 ou01 od00 ou02 od03 ss_0 ad0 tk10 tk13 w0a1 cq0
-ea0 w0a3 od02 w0a2 od01 sj0 w0b0 tk12 w0b1 w0b2 j0a1 w0b3 tk11 j0a3 j0a2 fa0 ca03 ca01 j0b3 ca00 au00 j0b1 j0b0 j0b2 au01 tc11 ca02 au02 cj01
-au03 sa0 cj00 cj02 mh01 lc03 cj03 lc02 lc00 lc01 tc10 mh02 mh00 tc12 mh03 ld02 ld01 tc13 ld03 mq0 tp00c tp00s tp01c tp01s sc10 sc11 pm10 du10
-pm11 du11 dc10 du13 sg1 du12 l1a1 l1a2 l1a3 dc11 l1b2 l1b0 dc12 l1b3 l1b1 dc13 sh11 sl1 al1 sh10 rb1 sh12 sh13 co12 co10 sq1 co11 co13 sc_1
-ou12 ou13 ou11 ou10 af1 ca10 ca12 od12 ss_1 ad1 cq10 od13 cq13 cq11 ca11 cq12 so1 ca13 sj1 ea1 fa1 od11 jl1 sa1 od10 cj13 lc10 cj12 lc12 lc13
-lc11 cj10 qw au10 cj11 ld13 au12 ld11 ld12 au13 mh10 au11 mh12 mh13 mh11 mq1 tp10c tp10s tp11c tp11s sc20 sc21 pm20 du20 pm21 du22 dc20 du21
-sg2 du23 l2a1 l2a2 l2a3 dc22 l2b1 l2b3 dc23 l2b0 l2b2 dc21 sh22 sl2 al2 sh20 rb2 sh23 sh21 ch co20 co21 sq2 co22 co23 sc_2 ou22 ou23 ou20 ou21
-af2 ca20 ca22 od22 ss_2 ad2 cq22 ca21 cq20 cq23 od23 cq21 so2 ca23 sj2 ea2 fa2 od21 jl2 sa2 od20 cj23 lc21 cj22 lc22 lc20 lc23 cj20 au22 cj21
-ld21 au23 ld22 au21 mh22 ld23 au20 mh23 y0 mh21 mh20 y1 mq2 yc0 yc1 tp20c y2 tp20s tp21c yc2 oc0 tp21s yp1 oc1 yp0 os0 os1 oy1 oy0 os3 os2"""
+ORDER = """z03 h0 z00 z02 pidx pand pblk lx0 z01 qc qd qx0 repi rep lk0 z1 e1 tk01 lk1 ejc qk0 t0c qk1 t0s sc00 e0 uc e2 lx1 e3 z2 tc01 eac dv01 dd01 pm00
+qx1 e4 row t2c m5a lw tk00 tk02 us tc02 sg0 l0a2 l0a3 tc00 du01 dc01 du03 l0a1 l0b1 l0b0 l0b2 l0b3 du02 dc02 dv02 sh01 dc03 dd02 sl0 sh02 tb0 du00 dc00
+sh00 sg0x sh03 sx0 rb0 co02 eoc m5c m6a co00 ax0 co03 al0 co01 m6c m6b m5b sq0 ou01 od01 ca03 t1c cq0 zq0 sj0 j0a2 so0 ca00 j0a3 fa0 ca02 sc_0 j0a1 j0b1
+j0b3 j0b2 j0b0 ss_0 ca01 ea0 sa0 ou00 od00 cj00 ou03 ou02 tk11 od02 od03 lc00 ad0 lc01 lc03 lc02 tk10 au00 mh00 cj02 au02 mh02 cj01 au01 mh01 au03 cj03
+mh03 tb1 tk12 ld03 ld01 ld02 tc10 tc11 t1s mq0 qw tp00c tp00s sc10 tp01s tc12 t2s tp01c sc11 du11 dc11 pm10 pm11 sg1 l1a1 dv11 dd11 du10 dc10 du13 sl1
+dv12 du12 al1 l1a2 l1a3 l1b2 l1b3 l1b0 l1b1 sh11 sh10 dd12 dc13 dc12 sh12 sg1x sx1 sh13 rb1 co13 ax1 sq1 sc_1 co11 co10 cq1 co12 ca12 ca10 sj1 j1a3 so1
+j1a1 ca13 fa1 j1a2 j1b0 j1b1 j1b3 j1b2 ea1 ca11 ss_1 sa1 ou11 ou10 od10 ad1 ou12 od12 cp1s od11 cp1c ou13 lc12 lc10 lc11 lc13 cj12 ld11 cj10 au10 mh10
+au12 mh12 au13 au11 cj11 mh11 ld13 ld12 mh13 mq1 tp10s zq1 tp10c sc20 tp11s tp11c sc21 du22 dc22 dv21 pm20 pm21 sg2 du20 du21 tb2 du23 dc21 dd21 dc20
+l2a3 l2a1 l2a2 l2b0 l2b3 l2b1 l2b2 sh21 dc23 dv22 sl2 dd22 sx2 sh22 sh20 al2 sg2x sh23 rb2 co21 co22 co23 co20 ax2 ca20 ca21 sq2 cq2 sj2 j2a3 sc_2 j2a2
+ca23 so2 j2a1 ca22 fa2 j2b2 j2b1 j2b0 j2b3 ea2 sa2 ou20 ss_2 ou21 ou22 od20 od21 ch y0 cp2s cp2c ou23 od22 ad2 au20 lc20 lc22 cj20 lc23 lc21 mh20 cj21
+cj22 au21 mh21 au23 mh23 au22 mh22 y1 yc1 yc0 ld23 ld21 ld22 mq2 y2 tp21s tp20s tp20c yc2 yp0 oc0 tp21c os1 os3 yp1 oc1 os2 os0 oy0"""
+ONV = """m5a m5b dc01 dc02 l0a2 l0a3 co02 j0a3 cj00 ca00 ca02 dc10 dd11 l1a2 l1a3 co12 j1a1 cj12 ca13 dc20 dd21 l2a2 l2a3 co20 j2a1 cj20 ca22 yc2 yp1"""
+
+
+def on_vector(name):
+    return name in ONV.split()
 
 
 def X(name, a=0, b=None, step=1, part=ALL, cast=None, off=None):
@@ -91,8 +99,8 @@ def plan(g, T):
         c, s = X(buf, a, b), X(buf + "s", a, b)
         op(name, "V", vec.quantize_mx, (c, s, tile), {}, [c, s])
 
-    def mx(name, out, st, a, mv, c, n):
-        op(name, "P", ten.matmul_mx, (out, X(st, a, a + 128), X(st + "s", a, a + 128), X(mv, c, c + n), X(mv + "s", c, c + n), True, True), {}, [out])
+    def mx(name, out, st, a, mv, c, n, start=True, stop=True):
+        op(name, "P", ten.matmul_mx, (out, X(st, a, a + 128), X(st + "s", a, a + 128), X(mv, c, c + n), X(mv + "s", c, c + n), start, stop), {}, [out])
 
     def pick(name, out, a, b, win, c, d, off):
         V(name + "c", vec.tensor_copy, X(out, a, b, cast=dt.uint32), X(win, c, d, cast=dt.uint32, off=off))
@@ -107,31 +115,29 @@ def plan(g, T):
     def landed(name, sem, outs, sends):
         ops.append({"name": name, "q": None, "rd": [], "wr": outs, "sem": sem, "kind": "a", "sends": sends})
 
-    def copy(name, q, out, in_, f=1.0):
-        if q == "A":
+    def copy(name, out, in_, f=1.0):
+        if not on_vector(name):
             A(name, out, in_, **({} if f == 1.0 else {"scale": f}))
         elif f == 1.0:
             V(name, vec.tensor_copy, out, in_)
         else:
             V(name, vec.tensor_scalar, out, in_, f, None, ALU.mult)
 
-    def differ(name, q, out, row, plain, scaled):
-        if q in "Aa":
+    def differ(name, out, row, plain, scaled=None):
+        if scaled and not on_vector(name):
             A(name, out, row, ACTF.Square, bias=scaled, scale=-S)
         else:
             V(name, vec.tensor_scalar, out, row, plain, BIG, ALU.not_equal, ALU.mult)
 
-    def fill(name, q, out, n, value):
-        if q == "G":
-            iota(name, out, [[0, n]], int(value))
-        elif q == "V":
+    def fill(name, out, n, value):
+        if on_vector(name):
             V(name, vec.memset, out, float(value))
         else:
             A(name, out, X("z", 0, n), scale=0.0, bias=float(value))
 
     def spread(name, out, buf, c, add=None):
         for k in range(1, 4):
-            copy("%sa%d" % (name, k), CFG["la"][k - 1], X(buf, c + k, c + k + 1, part=block(0)), X(buf, c, c + 1, part=block(k)))
+            copy("%sa%d" % (name, k), X(buf, c + k, c + k + 1, part=block(0)), X(buf, c, c + 1, part=block(k)))
         for k in range(4):
             if add is None:
                 V("%sb%d" % (name, k), vec.tensor_copy, X(out, part=block(k)), X(buf, c, c + 4, part=block(0)))
@@ -146,7 +152,7 @@ def plan(g, T):
 
     dma("lx0", "S", "lx0", X("h", 0, 256), T.x[:, 0:256])
     for m in range(2):
-        dma("lk%d" % m, CFG["lk"][m], "lk%d" % m, X("kt", 512 * m, 512 * m + 512), T.kb[:, 512 * m:512 * m + 512])
+        dma("lk%d" % m, "S", "lk%d" % m, X("kt", 512 * m, 512 * m + 512), T.kb[:, 512 * m:512 * m + 512])
     dma("lx1", "S", "lx1", X("xt"), T.x[:, 256:768])
     dma("lw", "S", "lw", X("wt"), T.w[:])
 
@@ -157,85 +163,100 @@ def plan(g, T):
     V("h0", vec.memset, X("h", 256, 512), 0.0)
     for t in range(4):
         quant("e%d" % t, "e", 128 * t, 128 * t + 128, X("z", 3 - t, 515 - t))
+    copy("z2", X("z2", 3 - BT, 515 - BT), X("z", 3 - BT, 515 - BT), 0.5)
+    quant("e4", "e", 512, 640, X("z2", 3 - BT, 515 - BT))
     quant("qx0", "xq", 0, 128, X("h", 0, 512))
     for m in range(2):
         quant("qk%d" % m, "win0", TB + 128 * m, TB + 128 * m + 128, X("kt", 512 * m, 512 * m + 512))
     V("pand", vec.tensor_scalar, X("pand", 0, 1), X("pidx"), 1, 15, ALU.logical_shift_right, ALU.bitwise_and)
     V("pblk", vec.tensor_scalar, X("pand", 1, 2), X("pidx"), 192, None, ALU.bitwise_and)
-    V("qc", vec.tensor_copy, X("qc"), X("pand"))
-    iota("repi", X("repi"), [[16, 8], [0, 2]])
+    V("qc", vec.tensor_copy, X("qc", 0, 1), X("pand", 0, 1))
+    V("qd", vec.tensor_copy, X("qc", 1, 2), X("pand", 1, 2))
+    iota("repi", X("repi"), [[16, 4], [0, 2]])
     V("rep", vec.tensor_scalar, X("rep"), X("repi"), X("qc", 0, 1), None, ALU.add)
-    pick("t0", "tr", 0, 128, "xq", 0, 128, X("rep", 0, 8))
+    pick("t0", "tr", 0, 128, "xq", 0, 128, X("rep"))
     iota("row", X("row"), [[1, 256]])
     V("uc", vec.tensor_scalar, X("uc"), X("repi", 0, 8, 2), X("qc", 0, 1), X("qc", 1, 2), ALU.add, ALU.add)
     A("us", X("us"), X("uc"), scale=S)
     A("eoc", X("eo", 64, 260, 65), X("uc"))
     for name, w, end in (("m5", 65, -65), ("m6", 66, -129)):
-        fill(name + "a", CFG["k"][0], X(name), 4 * w, -1)
-        fill(name + "b", CFG["k"][1], X(name, 0, 4 * w, w), 4, HUGE)
-        fill(name + "c", CFG["k"][1], X(name, 64, 4 * w, w), 4, end)
-    fill("ejc", CFG["k"][2], X("ej", 64, 260, 65), 4, -64)
-    fill("eac", CFG["k"][2], X("ea", 64, 264, 66), 4, HUGE)
+        fill(name + "a", X(name), 4 * w, -1)
+        fill(name + "b", X(name, 0, 4 * w, w), 4, HUGE)
+        fill(name + "c", X(name, 64, 4 * w, w), 4, end)
+    fill("ejc", X("ej", 64, 260, 65), 4, -64)
+    fill("eac", X("ea", 64, 264, 66), 4, HUGE)
     quant("qx1", "xq", 128, 256, X("xt"))
-    pick("t1", "tr", 128, 384, "xq", 128, 256, X("rep"))
+    for b in (1, 2):
+        pick("t%d" % b, "tr", 128 * b, 128 * b + 128, "xq", 64 * b + 64, 64 * b + 128, X("rep"))
     quant("qw", "wq", 0, 128, X("wt"))
 
     for b in range(R):
         W, N, n = "win%d" % b, "win%d" % (b + 1), str(b)
         wb, wa, jl, ll, wc, wr = [nm + n for nm in ("wb", "wa", "jl", "ll", "wc", "wr")]
-        raw = CFG["raw"][b] == "1"
         rb = X("rb", 64 * b, 64 * b + 64)
 
-        for m in range(2):
-            mx("sc%d%d" % (b, m), bank("pb", m, 0, 128), "tr", 128 * b, W, TB + 128 * m, 128)
-            V("pm%d%d" % (b, m), vec.tensor_tensor_scan, X("pm", 128 * m, 128 * m + 128), X("h", 256, 384), bank("pb", m, 0, 128),
-              X("pm", 127, 128) if m else -1.0e29, ALU.add, ALU.max)
+        for m in range(2 if CUT[b] < 256 else 1):
+            a, c = (CUT[b], 256) if m else (0, CUT[b])
+            u = max(c - a, 128)
+            mx("sc%d%d" % (b, m), bank("pb", m, 0, u), "tr", 128 * b, W, TB + c - u, u)
+            V("pm%d%d" % (b, m), vec.tensor_tensor_scan, X("pm", a, c), X("h", 256, 256 + c - a), bank("pb", m, u - c + a, u),
+              X("pm", a - 1, a) if m else -1.0e29, ALU.add, ALU.max)
         for t in range(4):
-            if b < 2:
+            if t == BT:
+                mx("tb" + n, bank("pa", t, 0, 128), "e", 512, "xq", 128 * min(b, 1), 128)
+            elif b < 2:
                 mx("tk%d%d" % (b, t), bank("pa", t, 0, 128), "e", 128 * t, "xq", 128 * b, 128)
-                copy("tc%d%d" % (b, t), CFG["tc"][t], X("tk%d" % t, 64 * b, 128 * b + 64), bank("pa", t, 0, 64 * b + 64), 0.5)
-            mx("du%d%d" % (b, t), bank("pa", t, 0, 256), "e", 128 * t, W, TB, 256)
-            copy("dc%d%d" % (b, t), CFG["dc"][4 * b + t], X("dk%d" % t), bank("pa", t, 0, 256), 1.5)
+                copy("tc%d%d" % (b, t), X("tk%d" % t, 64 * b, 128 * b + 64), bank("pa", t, 0, 64 * b + 64), 0.5)
+            if t not in HALVED:
+                u = bank("pb", 3, 0, 256) if t == BT else bank("pa", t, 0, 256)
+                mx("du%d%d" % (b, t), u, "e", 128 * t, W, TB, 256)
+                copy("dc%d%d" % (b, t), X("dk%d" % t), u, 1.5)
+            else:
+                for m in range(2):
+                    u = bank("pb", 2, 0, 128) if m else bank("pa", t, 0, 128)
+                    mx("d%s%d%d" % ("uv"[m], b, t), u, "e", 128 * t, W, TB + 128 * m, 128)
+                    copy("d%s%d%d" % ("cd"[m], b, t), X("dk%d" % t, 128 * m, 128 * m + 128), u, 1.5)
         A("sg" + n, X("sg"), X("pm"), ACTF.Sign, bias=X("pm", 255, 256), scale=-1.0, accum_out=X(wc, 0, 1))
         spread("l" + n, wb, wc, 0)
-        if raw:
-            send("sl" + n, "rl" + n, X(wr, 0, 1), X(wc, 0, 1))
-        else:
-            send("sl" + n, "rl" + n, X(wa), X(wb))
+        send("sl" + n, "rl" + n, X(wr, 0, 1), X(wc, 0, 1))
+        send("sx" + n, "rx" + n, X(wa), X(wb))
 
         for t in range(4):
-            V("sh%d%d" % (b, t), vec.tensor_tensor, X("h", t, 256, 4), X("dk%d" % t, off=X(wb)), X("tk%d" % t, 64 * b, 64 * b + 64), ALU.add)
+            if t == BT:
+                A("sg%dx" % b, X("sx"), X("dk%d" % t, off=X(wb)))
+                V("sh%d%d" % (b, t), vec.tensor_tensor, X("h", t, 256, 4), bank("pa", t, 64 * (b // 2), 64 * (b // 2) + 64), X("sx"), ALU.add)
+            else:
+                V("sh%d%d" % (b, t), vec.tensor_tensor, X("h", t, 256, 4), X("dk%d" % t, off=X(wb)), X("tk%d" % t, 64 * b, 64 * b + 64), ALU.add)
         quant("sq" + n, W, 192, 320, X("h", 0, 512))
+        if CUT[b + 1] < 128:
+            quant("zq" + n, N, 192, 320, X("h", 0, 512))
         send("sc_" + n, "rd" + n, X(W, 128, 192, cast=dt.uint8), X(W, 192, 256, cast=dt.uint8))
         send("ss_" + n, "rd" + n, X(W + "s", 128, 192), X(W + "s", 192, 256))
 
         A("rb" + n, rb, X("row", off=X(wb)))
         for k in range(4):
-            differ("co%d%d" % (b, k), CFG["co"][4 * b + k], X("eo", 65 * k, 65 * k + 64), rb, X("uc", k, k + 1), X("us", k, k + 1))
+            differ("co%d%d" % (b, k), X("eo", 65 * k, 65 * k + 64), rb, X("uc", k, k + 1), X("us", k, k + 1))
         V("so" + n, vec.tensor_tensor_scan, X("so"), X("m5"), X("eo"), 0.0, ALU.add, ALU.min)
-        copy("ea" + n, CFG["ea"], X("ea", 65, 264, 66), X("so", 64, 260, 65))
+        copy("ea" + n, X("ea", 65, 264, 66), X("so", 64, 260, 65))
         V("fa" + n, vec.tensor_scalar, X("m6", 65, 264, 66), X("so", 64, 260, 65), 0.0, -64.0, ALU.is_lt, ALU.mult)
 
-        if raw:
-            landed("al" + n, "rl" + n, [X(wr)], ["sl" + n])
-            differ("cq" + n, "V", X("ej", 0, 64), rb, X(wr, 0, 1), None)
-            V("sj" + n, vec.tensor_tensor_scan, X("sk", 0, 65), X("m5", 0, 65), X("ej", 0, 65), 0.0, ALU.add, ALU.min)
-            spread("j" + n, jl, "sk", 64, 128.0)
-            spread("w" + n, wa, wr, 0)
-        else:
-            landed("al" + n, "rl" + n, [X(wa)], ["sl" + n])
-            V("af" + n, vec.tensor_copy, X("af"), X(wa))
-            for k in range(4):
-                differ("cq%d%d" % (b, k), "V", X("ej", 65 * k, 65 * k + 64), rb, X("af", k, k + 1), None)
-            V("sj" + n, vec.tensor_tensor_scan, X("sj"), X("m5"), X("ej"), 0.0, ALU.add, ALU.min)
-            V("jl" + n, vec.tensor_scalar, X(jl), X("sj", 64, 260, 65), 128.0, None, ALU.add)
+        landed("al" + n, "rl" + n, [X(wr)], ["sl" + n])
+        differ("cq" + n, X("ej", 0, 64), rb, X(wr, 0, 1))
+        V("sj" + n, vec.tensor_tensor_scan, X("sk", 0, 65), X("m5", 0, 65), X("ej", 0, 65), 0.0, ALU.add, ALU.min)
+        spread("j" + n, jl, "sk", 64, 128.0)
+        landed("ax" + n, "rx" + n, [X(wa)], ["sx" + n])
+        if SUMMED[b]:
+            pick("cp" + n, "tr", 0, 64, W, 192, 320, X(jl))
         for t in range(4):
-            mx("ou%d%d" % (b, t), bank("pa", t, 0, 128), "e", 128 * t, W, 192, 128)
-            copy("od%d%d" % (b, t), CFG["od"][4 * b + t], X("od%d" % t), bank("pa", t, 0, 65))
-            copy("cj%d%d" % (b, t), CFG["cj"][4 * b + t], X("cj%d" % t), X("od%d" % t, off=X(jl)))
+            if t in SUMMED[b]:
+                mx("ou%d%d" % (b, t), bank("pb", t, 0, 128), "e", 128 * t, "tr", 0, 128, True, False)
+            else:
+                mx("ou%d%d" % (b, t), bank("pa", t, 0, 128), "e", 128 * t, W, 192, 128)
+                copy("od%d%d" % (b, t), X("od%d" % t), bank("pa", t, 0, 65))
+                copy("cj%d%d" % (b, t), X("cj%d" % t), X("od%d" % t, off=X(jl)))
 
         for k in range(4):
-            differ("ca%d%d" % (b, k), CFG["ca"][4 * b + k], X("ea", 66 * k, 66 * k + 64), X("row", off=X(wa)), X("uc", k, k + 1), X("us", k, k + 1))
+            differ("ca%d%d" % (b, k), X("ea", 66 * k, 66 * k + 64), X("row", off=X(wa)), X("uc", k, k + 1), X("us", k, k + 1))
         V("sa" + n, vec.tensor_tensor_scan, X("sa"), X("m6"), X("ea"), 0.0, ALU.add, ALU.min)
         for k in range(4):
             V("lc%d%d" % (b, k), vec.tensor_scalar, X(ll, 4 * k, 4 * k + 4, part=block(0)), X("sa", 65, 264, 66, part=block(k)), 256.0, None, ALU.add)
@@ -244,23 +265,27 @@ def plan(g, T):
 
         landed("ad" + n, "rd" + n, [X(W, 128, 192), X(W + "s", 128, 192)], ["sc_" + n, "ss_" + n])
         for t in range(4):
-            mx("au%d%d" % (b, t), bank("pb", t, 0, 128), "e", 128 * t, W, 128, 128)
-            V("mh%d%d" % (b, t), vec.tensor_tensor, X("h", 512 + t, 768, 4), bank("pb", t, 0, 64), X("cj%d" % t), ALU.add)
+            mx("au%d%d" % (b, t), bank("pb", t, 0, 128), "e", 128 * t, W, 128, 128, t not in SUMMED[b], True)
+            if t in SUMMED[b]:
+                copy("mh%d%d" % (b, t), X("h", 512 + t, 768, 4), bank("pb", t, 0, 64))
+            else:
+                V("mh%d%d" % (b, t), vec.tensor_tensor, X("h", 512 + t, 768, 4), bank("pb", t, 0, 64), X("cj%d" % t), ALU.add)
         quant("mq" + n, W, 0, 128, X("h", 256, 768))
         c = TB if b < R - 1 else 0
         for m in range(2):
-            pick("tp%d%d" % (b, m), N, c + 128 * m, c + 128 * m + 128, W, 64, 576, X(ll, 8 * m, 8 * m + 8))
+            u, v = (CUT[b + 1], 256) if m else (0, CUT[b + 1])
+            pick("tp%d%d" % (b, m), N, c + u, c + v, W, 64, 576, X(ll, u // 16, v // 16))
 
     dma("ch", "S", "st", T.ch[:], X("rb", part=(0, 1)))
     for i, (a, c, u) in enumerate(((TB, 576, 0), (128, 256, 0), (0, 128, 64))):
         mx("y%d" % i, bank("pa", i, 0, c - a), "wq", 0, W, a, c - a)
-        copy("yc%d" % i, CFG["y"][i], X("yw", a + u - 64, c - 64), bank("pa", i, u, c - a))
+        copy("yc%d" % i, X("yw", a + u - 64, c - 64), bank("pa", i, u, c - a))
     for m in range(2):
-        copy("yp%d" % m, CFG["y"][2 + m], X("yt", 128 * m, 128 * m + 128), X("yw", off=X(ll, 8 * m, 8 * m + 8)))
-        dma("oy%d" % m, CFG["o"][m], "st", T.y[:, 128 * m:128 * m + 128], X("yt", 128 * m, 128 * m + 128))
-        dma("oc%d" % m, CFG["oc"][m], "st", T.oc[:, 512 * m:512 * m + 512], X(N, 128 * m, 128 * m + 128, cast=dt.uint8))
+        copy("yp%d" % m, X("yt", 128 * m, 128 * m + 128), X("yw", off=X(ll, 8 * m, 8 * m + 8)))
+        dma("oc%d" % m, "S", "st", T.oc[:, 512 * m:512 * m + 512], X(N, 128 * m, 128 * m + 128, cast=dt.uint8))
+    dma("oy0", "S", "st", T.y[:], X("yt"))
     for k in range(4):
-        dma("os%d" % k, CFG["o"][2 + k], "st", T.osc[4 * k:4 * k + 4, :], X(N + "s", part=(32 * k, 32 * k + 4)))
+        dma("os%d" % k, STORES[k], "st", T.osc[4 * k:4 * k + 4, :], X(N + "s", part=(32 * k, 32 * k + 4)))
 
     for i, o in enumerate(ops):
         o["deps"] = []
@@ -279,7 +304,7 @@ def rank_program(g, core, T, topo):
         return
     ops = plan(g, T)
     by_name = {o["name"]: o for o in ops}
-    order = ORDER.split() if ORDER else [o["name"] for o in ops]
+    order = ORDER.split()
     queues = {"V": g.vector, "A": g.scalar, "P": g.tensor, "G": g, "S": g.sync}
     known = {q: {} for q in queues}
     count, token, total, waited = {}, {}, {}, {}

from concourse.mybir import dt, AluOpType, ActivationFunctionType

ALU = AluOpType
ACTF = ActivationFunctionType
R = 3
CUT = (256, 64, 64, 128)
HALVED = (1, 2)
BT = 3
SUMMED = ((), (3,), (3,))
STORES = "SSAA"
S = 32.0
BIG = S * S
HUGE = 4096.0
TB = 320
ALL = (0, 128)

X4 = "float8_e4m3fn_x4"
SCRATCH = {"pa": ("psum", [128, 2048], "float32"), "pb": ("psum", [128, 2048], "float32"),
           "pidx": ("sbuf", [128, 1], "int32"), "pand": ("sbuf", [128, 2], "int32"), "rep": ("sbuf", [128, 8], "uint16")}
for _n, _w in (("xt", 512), ("kt", 1024), ("wt", 512), ("z", 516), ("z2", 516), ("h", 768), ("sg", 256), ("m5", 260), ("m6", 264), ("eo", 260),
               ("so", 260), ("ej", 260), ("sk", 68), ("ea", 264), ("sa", 264)):
    SCRATCH[_n] = ("sbuf", [128, _w], "bfloat16")
for _n, _w in (("qc", 2), ("row", 256), ("pm", 256), ("repi", 8), ("uc", 4), ("us", 4), ("rb", 192), ("yw", 512), ("yt", 256), ("sx", 64)):
    SCRATCH[_n] = ("sbuf", [128, _w], "float32")
for _t in range(4):
    for _n, _w in (("dk", 256), ("tk", 192), ("od", 65), ("cj", 64)):
        SCRATCH["%s%d" % (_n, _t)] = ("sbuf", [128, _w], "float32")
for _n, _w in (("e", 640), ("xq", 256), ("tr", 384), ("wq", 128), ("win0", 576), ("win1", 576), ("win2", 576), ("win3", 256)):
    SCRATCH[_n] = ("sbuf", [128, _w], X4)
    SCRATCH[_n + "s"] = ("sbuf", [128, _w], "uint8")
for _b in range(R):
    for _n, _w in (("wb", 4), ("wa", 4), ("jl", 4), ("ll", 16)):
        SCRATCH["%s%d" % (_n, _b)] = ("sbuf", [128, _w], "uint16")
    for _n in ("wc", "wr"):
        SCRATCH["%s%d" % (_n, _b)] = ("sbuf", [128, 4], "float32")

SEMAPHORES = ["cV", "cA", "cP", "cG", "lx0", "lx1", "lk0", "lk1", "lw", "st", "loc"]
for _b in range(R):
    SEMAPHORES += ["rl%d" % _b, "rd%d" % _b, "rx%d" % _b]

ORDER = """z03 h0 z00 z02 pidx pand pblk lx0 z01 qc qd qx0 repi rep lk0 z1 e1 tk01 lk1 ejc qk0 t0c qk1 t0s sc00 e0 uc e2 lx1 e3 z2 tc01 eac dv01 dd01 pm00
qx1 e4 row t2c m5a lw tk00 tk02 us tc02 sg0 l0a2 l0a3 tc00 du01 dc01 du03 l0a1 l0b1 l0b0 l0b2 l0b3 du02 dc02 dv02 sh01 dc03 dd02 sl0 sh02 tb0 du00 dc00
sh00 sg0x sh03 sx0 rb0 co02 eoc m5c m6a co00 ax0 co03 al0 co01 m6c m6b m5b sq0 ou01 od01 ca03 t1c cq0 zq0 sj0 j0a2 so0 ca00 j0a3 fa0 ca02 sc_0 j0a1 j0b1
j0b3 j0b2 j0b0 ss_0 ca01 ea0 sa0 ou00 od00 cj00 ou03 ou02 tk11 od02 od03 lc00 ad0 lc01 lc03 lc02 tk10 au00 mh00 cj02 au02 mh02 cj01 au01 mh01 au03 cj03
mh03 tb1 tk12 ld03 ld01 ld02 tc10 tc11 t1s mq0 qw tp00c tp00s sc10 tp01s tc12 t2s tp01c sc11 du11 dc11 pm10 pm11 sg1 l1a1 dv11 dd11 du10 dc10 du13 sl1
dv12 du12 al1 l1a2 l1a3 l1b2 l1b3 l1b0 l1b1 sh11 sh10 dd12 dc13 dc12 sh12 sg1x sx1 sh13 rb1 co13 ax1 sq1 sc_1 co11 co10 cq1 co12 ca12 ca10 sj1 j1a3 so1
j1a1 ca13 fa1 j1a2 j1b0 j1b1 j1b3 j1b2 ea1 ca11 ss_1 sa1 ou11 ou10 od10 ad1 ou12 od12 cp1s od11 cp1c ou13 lc12 lc10 lc11 lc13 cj12 ld11 cj10 au10 mh10
au12 mh12 au13 au11 cj11 mh11 ld13 ld12 mh13 mq1 tp10s zq1 tp10c sc20 tp11s tp11c sc21 du22 dc22 dv21 pm20 pm21 sg2 du20 du21 tb2 du23 dc21 dd21 dc20
l2a3 l2a1 l2a2 l2b0 l2b3 l2b1 l2b2 sh21 dc23 dv22 sl2 dd22 sx2 sh22 sh20 al2 sg2x sh23 rb2 co21 co22 co23 co20 ax2 ca20 ca21 sq2 cq2 sj2 j2a3 sc_2 j2a2
ca23 so2 j2a1 ca22 fa2 j2b2 j2b1 j2b0 j2b3 ea2 sa2 ou20 ss_2 ou21 ou22 od20 od21 ch y0 cp2s cp2c ou23 od22 ad2 au20 lc20 lc22 cj20 lc23 lc21 mh20 cj21
cj22 au21 mh21 au23 mh23 au22 mh22 y1 yc1 yc0 ld23 ld21 ld22 mq2 y2 tp21s tp20s tp20c yc2 yp0 oc0 tp21c os1 os3 yp1 oc1 os2 os0 oy0"""
ONV = """m5a m5b dc01 dc02 l0a2 l0a3 co02 j0a3 cj00 ca00 ca02 dc10 dd11 l1a2 l1a3 co12 j1a1 cj12 ca13 dc20 dd21 l2a2 l2a3 co20 j2a1 cj20 ca22 yc2 yp1"""


def on_vector(name):
    return name in ONV.split()


def X(name, a=0, b=None, step=1, part=ALL, cast=None, off=None):
    return ("view", name, a, SCRATCH[name][1][1] if b is None else b, step, part, cast, off)


def is_view(x):
    return isinstance(x, tuple) and len(x) == 8 and x[0] == "view"


def meets(x, y):
    if x[1] != y[1] or x[5][1] <= y[5][0] or y[5][1] <= x[5][0] or x[3] <= y[2] or y[3] <= x[2]:
        return False
    return x[4] == 1 and y[4] == 1 or bool(set(range(x[2], x[3], x[4])) & set(range(y[2], y[3], y[4])))


def same_bank(x, y):
    return x[1] == y[1] and SCRATCH[x[1]][0] == "psum" and x[2] // 512 == y[2] // 512


def plan(g, T):
    ops = []
    vec, act, ten = g.vector, g.scalar, g.tensor

    def op(name, q, fn, args, kw, outs, sem=None, kind="c"):
        views = [a for a in list(args) + list(kw.values()) if is_view(a)]
        reads = [a for a in views if not any(a is o for o in outs)] + [a[7] for a in views if a[7] is not None]
        ops.append({"name": name, "q": q, "fn": fn, "args": args, "kw": kw, "rd": reads, "wr": list(outs), "sem": sem, "kind": kind})

    def V(name, fn, out, *args):
        op(name, "V", fn, (out,) + args, {}, [out])

    def G(name, fn, out, *args, **kw):
        op(name, "G", fn, (out,) + args, kw, [out])

    def A(name, out, in_, func=ACTF.Copy, **kw):
        op(name, "A", act.activation, (out, in_, func), kw, [out] + ([kw["accum_out"]] if "accum_out" in kw else []))

    def iota(name, out, pattern, base=0):
        G(name, g.iota, out, pattern, base, 0, allow_small_or_imprecise_dtypes=True)

    def quant(name, buf, a, b, tile):
        c, s = X(buf, a, b), X(buf + "s", a, b)
        op(name, "V", vec.quantize_mx, (c, s, tile), {}, [c, s])

    def mx(name, out, st, a, mv, c, n, start=True, stop=True):
        op(name, "P", ten.matmul_mx, (out, X(st, a, a + 128), X(st + "s", a, a + 128), X(mv, c, c + n), X(mv + "s", c, c + n), start, stop), {}, [out])

    def pick(name, out, a, b, win, c, d, off):
        V(name + "c", vec.tensor_copy, X(out, a, b, cast=dt.uint32), X(win, c, d, cast=dt.uint32, off=off))
        A(name + "s", X(out + "s", a, b), X(win + "s", c, d, off=off))

    def dma(name, q, sem, out, in_):
        op(name, q, (g.sync if q == "S" else act).dma_start, (out, in_), {}, [out] if is_view(out) else [], sem, "d")

    def send(name, sem, out, in_):
        ops.append({"name": name, "q": "G", "args": (out, in_), "kw": {}, "rd": [in_], "wr": [], "sem": sem, "kind": "r"})

    def landed(name, sem, outs, sends):
        ops.append({"name": name, "q": None, "rd": [], "wr": outs, "sem": sem, "kind": "a", "sends": sends})

    def copy(name, out, in_, f=1.0):
        if not on_vector(name):
            A(name, out, in_, **({} if f == 1.0 else {"scale": f}))
        elif f == 1.0:
            V(name, vec.tensor_copy, out, in_)
        else:
            V(name, vec.tensor_scalar, out, in_, f, None, ALU.mult)

    def differ(name, out, row, plain, scaled=None):
        if scaled and not on_vector(name):
            A(name, out, row, ACTF.Square, bias=scaled, scale=-S)
        else:
            V(name, vec.tensor_scalar, out, row, plain, BIG, ALU.not_equal, ALU.mult)

    def fill(name, out, n, value):
        if on_vector(name):
            V(name, vec.memset, out, float(value))
        else:
            A(name, out, X("z", 0, n), scale=0.0, bias=float(value))

    def spread(name, out, buf, c, add=None):
        for k in range(1, 4):
            copy("%sa%d" % (name, k), X(buf, c + k, c + k + 1, part=block(0)), X(buf, c, c + 1, part=block(k)))
        for k in range(4):
            if add is None:
                V("%sb%d" % (name, k), vec.tensor_copy, X(out, part=block(k)), X(buf, c, c + 4, part=block(0)))
            else:
                V("%sb%d" % (name, k), vec.tensor_scalar, X(out, part=block(k)), X(buf, c, c + 4, part=block(0)), add, None, ALU.add)

    def bank(buf, t, a, b):
        return X(buf, 512 * t + a, 512 * t + b)

    def block(k):
        return (32 * k, 32 * k + 32)

    dma("lx0", "S", "lx0", X("h", 0, 256), T.x[:, 0:256])
    for m in range(2):
        dma("lk%d" % m, "S", "lk%d" % m, X("kt", 512 * m, 512 * m + 512), T.kb[:, 512 * m:512 * m + 512])
    dma("lx1", "S", "lx1", X("xt"), T.x[:, 256:768])
    dma("lw", "S", "lw", X("wt"), T.w[:])

    for t in range(4):
        V("z0%d" % t, vec.memset, X("z", t, 516, 4), 0.0)
    G("pidx", g.iota, X("pidx"), [[0, 1]], 0, 2)
    G("z1", g.affine_select, X("z", 3, 515, 4), X("z", 3, 515, 4), [[-1, 128]], ALU.not_equal, 0.5, 0, 1)
    V("h0", vec.memset, X("h", 256, 512), 0.0)
    for t in range(4):
        quant("e%d" % t, "e", 128 * t, 128 * t + 128, X("z", 3 - t, 515 - t))
    copy("z2", X("z2", 3 - BT, 515 - BT), X("z", 3 - BT, 515 - BT), 0.5)
    quant("e4", "e", 512, 640, X("z2", 3 - BT, 515 - BT))
    quant("qx0", "xq", 0, 128, X("h", 0, 512))
    for m in range(2):
        quant("qk%d" % m, "win0", TB + 128 * m, TB + 128 * m + 128, X("kt", 512 * m, 512 * m + 512))
    V("pand", vec.tensor_scalar, X("pand", 0, 1), X("pidx"), 1, 15, ALU.logical_shift_right, ALU.bitwise_and)
    V("pblk", vec.tensor_scalar, X("pand", 1, 2), X("pidx"), 192, None, ALU.bitwise_and)
    V("qc", vec.tensor_copy, X("qc", 0, 1), X("pand", 0, 1))
    V("qd", vec.tensor_copy, X("qc", 1, 2), X("pand", 1, 2))
    iota("repi", X("repi"), [[16, 4], [0, 2]])
    V("rep", vec.tensor_scalar, X("rep"), X("repi"), X("qc", 0, 1), None, ALU.add)
    pick("t0", "tr", 0, 128, "xq", 0, 128, X("rep"))
    iota("row", X("row"), [[1, 256]])
    V("uc", vec.tensor_scalar, X("uc"), X("repi", 0, 8, 2), X("qc", 0, 1), X("qc", 1, 2), ALU.add, ALU.add)
    A("us", X("us"), X("uc"), scale=S)
    A("eoc", X("eo", 64, 260, 65), X("uc"))
    for name, w, end in (("m5", 65, -65), ("m6", 66, -129)):
        fill(name + "a", X(name), 4 * w, -1)
        fill(name + "b", X(name, 0, 4 * w, w), 4, HUGE)
        fill(name + "c", X(name, 64, 4 * w, w), 4, end)
    fill("ejc", X("ej", 64, 260, 65), 4, -64)
    fill("eac", X("ea", 64, 264, 66), 4, HUGE)
    quant("qx1", "xq", 128, 256, X("xt"))
    for b in (1, 2):
        pick("t%d" % b, "tr", 128 * b, 128 * b + 128, "xq", 64 * b + 64, 64 * b + 128, X("rep"))
    quant("qw", "wq", 0, 128, X("wt"))

    for b in range(R):
        W, N, n = "win%d" % b, "win%d" % (b + 1), str(b)
        wb, wa, jl, ll, wc, wr = [nm + n for nm in ("wb", "wa", "jl", "ll", "wc", "wr")]
        rb = X("rb", 64 * b, 64 * b + 64)

        for m in range(2 if CUT[b] < 256 else 1):
            a, c = (CUT[b], 256) if m else (0, CUT[b])
            u = max(c - a, 128)
            mx("sc%d%d" % (b, m), bank("pb", m, 0, u), "tr", 128 * b, W, TB + c - u, u)
            V("pm%d%d" % (b, m), vec.tensor_tensor_scan, X("pm", a, c), X("h", 256, 256 + c - a), bank("pb", m, u - c + a, u),
              X("pm", a - 1, a) if m else -1.0e29, ALU.add, ALU.max)
        for t in range(4):
            if t == BT:
                mx("tb" + n, bank("pa", t, 0, 128), "e", 512, "xq", 128 * min(b, 1), 128)
            elif b < 2:
                mx("tk%d%d" % (b, t), bank("pa", t, 0, 128), "e", 128 * t, "xq", 128 * b, 128)
                copy("tc%d%d" % (b, t), X("tk%d" % t, 64 * b, 128 * b + 64), bank("pa", t, 0, 64 * b + 64), 0.5)
            if t not in HALVED:
                u = bank("pb", 3, 0, 256) if t == BT else bank("pa", t, 0, 256)
                mx("du%d%d" % (b, t), u, "e", 128 * t, W, TB, 256)
                copy("dc%d%d" % (b, t), X("dk%d" % t), u, 1.5)
            else:
                for m in range(2):
                    u = bank("pb", 2, 0, 128) if m else bank("pa", t, 0, 128)
                    mx("d%s%d%d" % ("uv"[m], b, t), u, "e", 128 * t, W, TB + 128 * m, 128)
                    copy("d%s%d%d" % ("cd"[m], b, t), X("dk%d" % t, 128 * m, 128 * m + 128), u, 1.5)
        A("sg" + n, X("sg"), X("pm"), ACTF.Sign, bias=X("pm", 255, 256), scale=-1.0, accum_out=X(wc, 0, 1))
        spread("l" + n, wb, wc, 0)
        send("sl" + n, "rl" + n, X(wr, 0, 1), X(wc, 0, 1))
        send("sx" + n, "rx" + n, X(wa), X(wb))

        for t in range(4):
            if t == BT:
                A("sg%dx" % b, X("sx"), X("dk%d" % t, off=X(wb)))
                V("sh%d%d" % (b, t), vec.tensor_tensor, X("h", t, 256, 4), bank("pa", t, 64 * (b // 2), 64 * (b // 2) + 64), X("sx"), ALU.add)
            else:
                V("sh%d%d" % (b, t), vec.tensor_tensor, X("h", t, 256, 4), X("dk%d" % t, off=X(wb)), X("tk%d" % t, 64 * b, 64 * b + 64), ALU.add)
        quant("sq" + n, W, 192, 320, X("h", 0, 512))
        if CUT[b + 1] < 128:
            quant("zq" + n, N, 192, 320, X("h", 0, 512))
        send("sc_" + n, "rd" + n, X(W, 128, 192, cast=dt.uint8), X(W, 192, 256, cast=dt.uint8))
        send("ss_" + n, "rd" + n, X(W + "s", 128, 192), X(W + "s", 192, 256))

        A("rb" + n, rb, X("row", off=X(wb)))
        for k in range(4):
            differ("co%d%d" % (b, k), X("eo", 65 * k, 65 * k + 64), rb, X("uc", k, k + 1), X("us", k, k + 1))
        V("so" + n, vec.tensor_tensor_scan, X("so"), X("m5"), X("eo"), 0.0, ALU.add, ALU.min)
        copy("ea" + n, X("ea", 65, 264, 66), X("so", 64, 260, 65))
        V("fa" + n, vec.tensor_scalar, X("m6", 65, 264, 66), X("so", 64, 260, 65), 0.0, -64.0, ALU.is_lt, ALU.mult)

        landed("al" + n, "rl" + n, [X(wr)], ["sl" + n])
        differ("cq" + n, X("ej", 0, 64), rb, X(wr, 0, 1))
        V("sj" + n, vec.tensor_tensor_scan, X("sk", 0, 65), X("m5", 0, 65), X("ej", 0, 65), 0.0, ALU.add, ALU.min)
        spread("j" + n, jl, "sk", 64, 128.0)
        landed("ax" + n, "rx" + n, [X(wa)], ["sx" + n])
        if SUMMED[b]:
            pick("cp" + n, "tr", 0, 64, W, 192, 320, X(jl))
        for t in range(4):
            if t in SUMMED[b]:
                mx("ou%d%d" % (b, t), bank("pb", t, 0, 128), "e", 128 * t, "tr", 0, 128, True, False)
            else:
                mx("ou%d%d" % (b, t), bank("pa", t, 0, 128), "e", 128 * t, W, 192, 128)
                copy("od%d%d" % (b, t), X("od%d" % t), bank("pa", t, 0, 65))
                copy("cj%d%d" % (b, t), X("cj%d" % t), X("od%d" % t, off=X(jl)))

        for k in range(4):
            differ("ca%d%d" % (b, k), X("ea", 66 * k, 66 * k + 64), X("row", off=X(wa)), X("uc", k, k + 1), X("us", k, k + 1))
        V("sa" + n, vec.tensor_tensor_scan, X("sa"), X("m6"), X("ea"), 0.0, ALU.add, ALU.min)
        for k in range(4):
            V("lc%d%d" % (b, k), vec.tensor_scalar, X(ll, 4 * k, 4 * k + 4, part=block(0)), X("sa", 65, 264, 66, part=block(k)), 256.0, None, ALU.add)
        for k in range(1, 4):
            V("ld%d%d" % (b, k), vec.tensor_copy, X(ll, part=block(k)), X(ll, part=block(0)))

        landed("ad" + n, "rd" + n, [X(W, 128, 192), X(W + "s", 128, 192)], ["sc_" + n, "ss_" + n])
        for t in range(4):
            mx("au%d%d" % (b, t), bank("pb", t, 0, 128), "e", 128 * t, W, 128, 128, t not in SUMMED[b], True)
            if t in SUMMED[b]:
                copy("mh%d%d" % (b, t), X("h", 512 + t, 768, 4), bank("pb", t, 0, 64))
            else:
                V("mh%d%d" % (b, t), vec.tensor_tensor, X("h", 512 + t, 768, 4), bank("pb", t, 0, 64), X("cj%d" % t), ALU.add)
        quant("mq" + n, W, 0, 128, X("h", 256, 768))
        c = TB if b < R - 1 else 0
        for m in range(2):
            u, v = (CUT[b + 1], 256) if m else (0, CUT[b + 1])
            pick("tp%d%d" % (b, m), N, c + u, c + v, W, 64, 576, X(ll, u // 16, v // 16))

    dma("ch", "S", "st", T.ch[:], X("rb", part=(0, 1)))
    for i, (a, c, u) in enumerate(((TB, 576, 0), (128, 256, 0), (0, 128, 64))):
        mx("y%d" % i, bank("pa", i, 0, c - a), "wq", 0, W, a, c - a)
        copy("yc%d" % i, X("yw", a + u - 64, c - 64), bank("pa", i, u, c - a))
    for m in range(2):
        copy("yp%d" % m, X("yt", 128 * m, 128 * m + 128), X("yw", off=X(ll, 8 * m, 8 * m + 8)))
        dma("oc%d" % m, "S", "st", T.oc[:, 512 * m:512 * m + 512], X(N, 128 * m, 128 * m + 128, cast=dt.uint8))
    dma("oy0", "S", "st", T.y[:], X("yt"))
    for k in range(4):
        dma("os%d" % k, STORES[k], "st", T.osc[4 * k:4 * k + 4, :], X(N + "s", part=(32 * k, 32 * k + 4)))

    for i, o in enumerate(ops):
        o["deps"] = []
        for e in ops[:i]:
            if o["q"] == "P" and e["q"] == "P":
                continue
            if (any(meets(x, y) for x in o["rd"] + o["wr"] for y in e["wr"]) or any(meets(x, y) for x in o["wr"] for y in e["rd"])
                    or o["q"] != e["q"] and any(same_bank(x, y) for x in o["rd"] + o["wr"] for y in e["rd"] + e["wr"])):
                o["deps"].append(e["name"])
    return ops


def rank_program(g, core, T, topo):
    rank = T.rank_of(core)
    if rank is None:
        return
    ops = plan(g, T)
    by_name = {o["name"]: o for o in ops}
    order = ORDER.split()
    queues = {"V": g.vector, "A": g.scalar, "P": g.tensor, "G": g, "S": g.sync}
    known = {q: {} for q in queues}
    count, token, total, waited = {}, {}, {}, {}
    to = []
    for b in range(R):
        dst = T.cores[rank ^ (1 << b)]
        rid, pid, _s = topo.addr(dst)
        to.append((pid, rid, topo.mask(core, dst), len(topo.engines(core, dst))))
    for o in ops:
        if o["kind"] == "d":
            total[o["sem"]] = total.get(o["sem"], 0) + 16
        if o["kind"] == "r":
            total[o["sem"]] = total.get(o["sem"], 0) + to[int(o["sem"][-1])][3]
            total["loc"] = total.get("loc", 0) + to[int(o["sem"][-1])][3]

    def real(x):
        if not is_view(x):
            return x
        _v, name, a, b, step, part, cast, off = x
        ap = T[name][slice(None) if part == ALL else slice(part[0], part[1]), slice(a, b) if step == 1 else slice(a, b, step)]
        if cast is not None:
            ap = ap.bitcast(cast)
        return ap if off is None else ap.indirect(real(off))

    for name in order:
        o = by_name[name]
        q = o["q"]
        if q is None:
            token[name] = (o["sem"], total[o["sem"]], {})
            continue
        wants = [token[d] for d in o["deps"]]
        most = {}
        for sem, val, through in wants:
            most[sem] = max(most.get(sem, 0), val)
        for sem, val in most.items():
            if known[q].get(sem, 0) < val and not any(w[2].get(sem, 0) >= val for w in wants):
                queues[q].wait_ge(T.sem[sem], val)
                waited[sem] = max(waited.get(sem, 0), val)
        for sem, val, through in wants:
            for s, v in list(through.items()) + [(sem, val)]:
                known[q][s] = max(known[q].get(s, 0), v)
        args, kw = [real(a) for a in o["args"]], {k: real(a) for k, a in o["kw"].items()}
        if o["kind"] == "r":
            pid, rid, mask, _n = to[int(o["sem"][-1])]
            g.remote_dma(args[0], args[1], T.sem[o["sem"]], T.sem.loc, pid, rid, mask)
        elif o["kind"] == "d":
            o["fn"](*args).then_inc(T.sem[o["sem"]], 16)
            token[name] = (o["sem"], total[o["sem"]], dict(known[q]))
        else:
            total["c" + q] = count[q] = count.get(q, 0) + 1
            o["fn"](*args, **kw).then_inc(T.sem["c" + q], 1)
            token[name] = ("c" + q, count[q], dict(known[q]))
    for sem, val in total.items():
        if waited.get(sem, 0) < val:
            (g if sem == "loc" else g.sync).wait_ge(T.sem[sem], val)
